import numpy as np
import ml_dtypes


def mxq(x, axis, fmt="e4m3"):
    dtype, down = {"e4m3": (ml_dtypes.float8_e4m3fn, 7), "e5m2": (ml_dtypes.float8_e5m2, 14)}[fmt]
    v = np.moveaxis(np.asarray(x, np.float32).astype(ml_dtypes.bfloat16).astype(np.float64), axis, -1)
    blocks = v.reshape(v.shape[:-1] + (-1, 32))
    amax = np.abs(blocks).max(-1, keepdims=True)
    byte = np.maximum(np.where(amax > 0, np.frexp(amax)[1] - 1 + 127, 0) - down, 1)
    scale = np.exp2(byte - 127.0)
    codes = (blocks / scale).astype(np.float32).astype(dtype).astype(np.float64)
    return np.moveaxis((codes * scale).reshape(v.shape), -1, axis)


WIDE = False


def mx_kscale(k):
    if not WIDE:
        return np.ones(k)
    levels = np.array([10, -10, 5, -5, 0])
    if k % 512:
        return np.exp2(np.random.permutation(np.resize(levels, k // 32))).repeat(32)
    a = np.empty((k // 512, 16))
    for p in range(k // 512):
        a[p, :8] = np.random.permutation(np.resize(levels, 8))
        for g in range(8):
            far = levels[np.abs(levels - a[p, g]) >= 10]
            a[p, g + 8] = far[np.random.randint(len(far))]
    return np.exp2(a.ravel()).repeat(32)


def f64(x):
    return np.asarray(x).astype(np.float64)


def striped(idx):
    return np.tile(idx.reshape(-1, 16).T, (8, 1)).astype(np.uint16)


def unstriped(offs):
    return offs[:16].T.reshape(-1).astype(np.int64)


E2M1 = np.array([0.0, 0.5, 1.0, 1.5, 2.0, 3.0, 4.0, 6.0, -0.0, -0.5, -1.0, -1.5, -2.0, -3.0, -4.0, -6.0])


def pack_weight(w, fmt):
    k, n = w.shape
    w = f64(np.asarray(w, np.float32).astype(ml_dtypes.bfloat16)).reshape(k // 32, 32, n)
    amax = np.abs(w).max(1)
    if fmt == "e4m3":
        byte = np.frexp(amax)[1] - 1 + 127 - 7
    else:
        mant, ex = np.frexp(amax / 6.0)
        byte = np.where(mant > 0.5, ex, ex - 1) + 127
    byte = np.clip(np.where(amax > 0, byte, 1), 1, 254)
    scaled = (w * np.exp2(127.0 - byte)[:, None, :]).reshape(k, n).astype(np.float32)
    by_word = np.ascontiguousarray(scaled.reshape(k // 512, 128, 4, n).transpose(0, 1, 3, 2))
    if fmt == "e4m3":
        words = by_word.astype(ml_dtypes.float8_e4m3fn).view(np.uint8)
    else:
        c = by_word.astype(ml_dtypes.float4_e2m1fn).view(np.uint8) & 0xF
        words = (c[..., 0::2] | (c[..., 1::2] << 4)).reshape(k // 512, 128, 2 * n)
    return np.ascontiguousarray(words), np.ascontiguousarray(byte.astype(np.uint8).reshape(k // 512, 16, n))


def unpack_weight(words, scales, fmt):
    g, _, n = scales.shape
    words = np.ascontiguousarray(words).reshape(g, 128, n, -1)
    if fmt == "e4m3":
        vals = words.view(ml_dtypes.float8_e4m3fn).astype(np.float64)
    else:
        nib = np.empty((g, 128, n, 4), np.uint8)
        nib[..., 0::2] = words & 0xF
        nib[..., 1::2] = words >> 4
        vals = E2M1[nib]
    vals = vals * np.repeat(np.exp2(scales.astype(np.float64) - 127.0), 8, axis=1)[..., None]
    return vals.transpose(0, 1, 3, 2).reshape(g * 512, n)


def gelu(v):
    return 0.5 * v * (1.0 + np.tanh(np.sqrt(2.0 / np.pi) * (v + 0.044715 * v**3)))


K, H, N, T, S, P, P2 = 1024, 1024, 512, 2048, 1024, 512, 256

def setup_inputs():
    n = np.random.standard_normal
    s = mx_kscale(K)[:, None]
    u = mx_kscale(H)[:, None]
    tab_words, tab_scales = pack_weight(n((K, T)) * s, "e4m3")
    w1_words, w1_scales = pack_weight(0.9 * n((K, H)) / np.sqrt(K) / s, "e2m1")
    return {
        "tab_words": tab_words, "tab_scales": tab_scales,
        "offs": striped(np.random.permutation(T)[:S]),
        "w1_words": w1_words, "w1_scales": w1_scales,
        "gain": (np.exp(0.3 * n(H)) * u[:, 0]).astype(np.float32),
        "pos1": striped(np.random.permutation(S)[:P]),
        "pos2": striped(np.random.permutation(S)[:P]),
        "w2": (1.5 * n((H, N)) / np.sqrt(H) / u).astype(np.float32),
        "pos3": striped(np.random.permutation(P)[:P2]),
        "pos4": striped(np.random.permutation(P)[:P2]),
    }

def reference(tab_words, tab_scales, offs, w1_words, w1_scales, gain, pos1, pos2, w2, pos3, pos4):
    v = unpack_weight(tab_words, tab_scales, "e4m3")[:, unstriped(offs)]
    w1 = unpack_weight(w1_words, w1_scales, "e2m1")
    d = w1.T @ v
    h = f64(gain)[:, None] * np.exp(-np.square(d))
    z = np.maximum(h[:, unstriped(pos1)], h[:, unstriped(pos2)])
    y = mxq(f64(w2), 0, "e4m3").T @ mxq(z, 0, "e4m3")
    out = y[:, unstriped(pos3)] / (1.0 + np.abs(y[:, unstriped(pos4)]))
    return out

@@ -1,0 +1,225 @@
+from contextlib import ExitStack
+
+import concourse.mybir as mybir
+from concourse.masks import make_identity
+
+K, H, N, T, S, P1, P2 = 1024, 1024, 512, 2048, 1024, 512, 256
+FLOPS = 2 * K * H * S + 2 * H * N * P1
+
+F32 = mybir.dt.float32
+BF16 = mybir.dt.bfloat16
+I32 = mybir.dt.int32
+U32 = mybir.dt.uint32
+U16 = mybir.dt.uint16
+U8 = mybir.dt.uint8
+FP8X4 = mybir.dt.float8_e4m3fn_x4
+FP4X4 = mybir.dt.float4_e2m1fn_x4
+ACT = mybir.ActivationFunctionType
+ALU = mybir.AluOpType
+
+P = 128
+HALF = 512
+
+
+def tile_list_rumour_cascade_scores_kernel(
+    tc, tab_words, tab_scales, offs, w1_words, w1_scales, gain, pos1, pos2, w2, pos3, pos4, out
+):
+    nc = tc.nc
+    with ExitStack() as ctx:
+        keep = ctx.enter_context(tc.tile_pool(name="keep", bufs=1))
+        psum = ctx.enter_context(tc.psum_pool(name="psum", bufs=8))
+
+        def load_list(src, name):
+            lst = keep.tile([P, src.shape[1]], U16, name=name)
+            nc.sync.dma_start(lst[:], src)
+            return lst
+
+        tab_sc = keep.tile([P, T], U8, name="tab_sc", align_bytes=64)
+        for q in range(4):
+            nc.vector.memset(tab_sc[32 * q : 32 * q + 24, :].bitcast(I32), 0)
+        w1_sc_raw = keep.tile([P, 2 * H], U8, name="w1_sc_raw", align_bytes=64)
+        nc.vector.memset(w1_sc_raw[:].bitcast(I32), 0)
+        v_sc = [keep.tile([P, S], U8, name=f"v_sc{a}", align_bytes=64) for a in range(2)]
+        for a in range(2):
+            nc.vector.memset(v_sc[a][96:128, :].bitcast(I32), 0)
+
+        offs_t = load_list(offs, "offs_t")
+        for q in range(4):
+            nc.sync.dma_start(
+                tab_sc[32 * q + 24 : 32 * q + 32, :].bitcast(I32), tab_scales[:, 4 * q : 4 * q + 4, :].bitcast(I32)
+            )
+        tab_w = [keep.tile([P, T], U32, name=f"tab_w{a}", align_bytes=64) for a in range(2)]
+        w1_raw = [keep.tile([P, 2 * H], U8, name=f"w1_raw{b}", align_bytes=64) for b in range(2)]
+        for a in range(2):
+            nc.sync.dma_start(tab_w[a][:].bitcast(I32), tab_words[a].rearrange("p t i -> p (t i)").bitcast(I32))
+            nc.sync.dma_start(
+                w1_raw[a][:].bitcast(I32).rearrange("p (a c) -> p a c", a=2),
+                w1_words[:, :, H * a : H * (a + 1)].rearrange("a p c -> p a c").bitcast(I32),
+            )
+        for q in range(4):
+            nc.scalar.dma_start(
+                w1_sc_raw[32 * q : 32 * q + 4, :].bitcast(I32).rearrange("p (a c) -> p a c", a=2),
+                w1_scales[:, 4 * q : 4 * q + 4, :].rearrange("a r c -> r a c").bitcast(I32),
+            )
+        gain_rows = keep.tile([P, P], F32, name="gain_rows")
+        nc.gpsimd.memset(gain_rows[:], 0.0)
+        for b in range(2):
+            nc.gpsimd.dma_start(
+                gain_rows[4 * b : 4 * (b + 1), :].rearrange("t (B i) -> t B i", i=8),
+                gain[HALF * b : HALF * (b + 1)].rearrange("(B t i) -> t B i", t=4, i=8),
+            )
+        ident = keep.tile([P, P], F32, name="ident")
+        make_identity(nc, ident[:])
+        gain_cols = psum.tile([P, P], F32, name="acc")
+        nc.tensor.transpose(gain_cols[:], gain_rows[:], ident[:])
+        log_gain = keep.tile([P, 8], F32, name="log_gain")
+        nc.scalar.activation(log_gain[:], gain_cols[:, 0:8], ACT.Ln)
+        pos1_t = load_list(pos1, "pos1_t")
+        pos2_t = load_list(pos2, "pos2_t")
+        w2_raw = []
+        for b in range(2):
+            raw = keep.tile([P, 4, N], F32, name=f"w2_raw{b}")
+            rows = w2[HALF * b : HALF * (b + 1), :].rearrange("(B t i) n -> t B i n", t=4, i=8)
+            for t in range(4):
+                nc.sync.dma_start(raw[:, t, :], rows[t])
+            w2_raw.append(raw)
+        pos3_t = load_list(pos3, "pos3_t")
+        pos4_t = load_list(pos4, "pos4_t")
+
+        picked_sc = keep.tile([P, S], U8, name="picked_sc", align_bytes=64)
+        nc.vector.tensor_copy(picked_sc[:], tab_sc[:].indirect(offs_t[:]))
+        for a in range(2):
+            first = 24 + 4 * a
+            nc.scalar.dma_start(v_sc[a][0:100, :].bitcast(I32), picked_sc[first : first + 100, :].bitcast(I32))
+        v_w0 = keep.tile([P, S], U32, name="v_w0", align_bytes=64)
+        nc.vector.tensor_copy(v_w0[:], tab_w[0][:].indirect(offs_t[:]))
+
+        w1_w, w1_sc = [], []
+
+        def order_w1(b):
+            words = keep.tile([P, 2 * 4 * 256], U8, name=f"w1_w{b}", align_bytes=64)
+            nc.vector.tensor_copy(
+                words[:].bitcast(I32).rearrange("p (a t B i) -> p a t B i", a=2, t=4, i=4),
+                w1_raw[b][:].bitcast(I32).rearrange("p (a B t i) -> p a t B i", a=2, t=4, i=4),
+            )
+            sc = keep.tile([P, 2 * 4 * 128], U8, name=f"w1_sc{b}", align_bytes=64)
+            nc.vector.tensor_copy(
+                sc[:].bitcast(I32).rearrange("p (a t B i) -> p a t B i", a=2, t=4, i=2),
+                w1_sc_raw[:].bitcast(I32).rearrange("p (a b B t i) -> p b a t B i", a=2, b=2, t=4, i=2)[:, b],
+            )
+            w1_w.append(words)
+            w1_sc.append(sc)
+
+        order_w1(0)
+        v_w1 = []
+        for u in range(2):
+            vw = keep.tile([P, HALF], U32, name=f"v_w1_{u}", align_bytes=64)
+            nc.vector.tensor_copy(vw[:], tab_w[1][:].indirect(offs_t[:, 32 * u : 32 * (u + 1)]))
+            v_w1.append(vw)
+        order_w1(1)
+
+        def moving(a, u):
+            if a == 0:
+                return v_w0[:, HALF * u : HALF * (u + 1)]
+            return v_w1[u][:]
+
+        def responses(b, t):
+            h = keep.tile([P, S], F32, name=f"h{b}{t}")
+            sq = keep.tile([P, S], F32, name="sq", tag=f"scratch{4 * b + t}", align_bytes=64)
+            bias = log_gain[:, 4 * b + t : 4 * b + t + 1]
+            for u in range(2):
+                cols = slice(HALF * u, HALF * (u + 1))
+                d = psum.tile([P, HALF], F32, name="acc")
+                for a in range(2):
+                    j = 4 * a + t
+                    nc.tensor.matmul_mx(
+                        out=d[:],
+                        lhsT=w1_w[b][:, 256 * j : 256 * (j + 1)].bitcast(FP4X4),
+                        lhsT_scale=w1_sc[b][:, 128 * j : 128 * (j + 1)],
+                        rhs=moving(a, u).bitcast(FP8X4),
+                        rhs_scale=v_sc[a][:, cols],
+                        start=(a == 0),
+                        stop=(a == 1),
+                    )
+                nc.scalar.activation(sq[:, cols], d[:], ACT.Square)
+                if b == 0 and t == 0:
+                    nc.scalar.activation(h[:, cols], sq[:, cols], ACT.Exp, bias=bias, scale=-1.0)
+            if b or t:
+                nc.scalar.activation(h[:], sq[:], ACT.Exp, bias=bias, scale=-1.0)
+            return h
+
+        def weave(ap3):
+            return ap3.rearrange("p t (c i) -> p c t i", i=4)
+
+        def woven(ap3):
+            return ap3.rearrange("p (c i) t -> p c t i", i=4)
+
+        w2_w = [keep.tile([P, N], U32, name=f"w2_w{b}", align_bytes=64) for b in range(2)]
+        w2_sc = [keep.tile([P, N], U8, name=f"w2_sc{b}", align_bytes=64) for b in range(2)]
+
+        def quantize_w2(b, cols, behind):
+            width = cols.stop - cols.start
+            grouped = keep.tile([P, width, 4], BF16, name="w2_g", tag=f"scratch{behind}", align_bytes=64)
+            nc.scalar.copy(woven(grouped[:]), weave(w2_raw[b][:, :, cols]))
+            nc.vector.quantize_mx(
+                out=w2_w[b][:, cols].bitcast(FP8X4),
+                scales=w2_sc[b][:, cols],
+                in_=grouped[:].rearrange("p n t -> p (n t)"),
+            )
+
+        w2_pieces = {3: (0, slice(0, 512)), 5: (1, slice(0, 256)), 7: (1, slice(256, 512))}
+        z_w, z_sc = {}, {}
+        for b in range(2):
+            g1 = keep.tile([P, 4, P1], F32, name=f"g1_{b}")
+            g2 = keep.tile([P, 4, P1], F32, name=f"g2_{b}")
+            z = keep.tile([P, P1, 4], BF16, name=f"z{b}", align_bytes=64)
+            hs = []
+            for t in range(4):
+                hs.append(responses(b, t))
+                if 4 * b + t in w2_pieces:
+                    quantize_w2(*w2_pieces[4 * b + t], 4 * b + t)
+                if b == 1 and t == 3:
+                    break
+                nc.vector.tensor_copy(g1[:, t, :], hs[t][:].indirect(pos1_t[:]))
+                nc.vector.tensor_copy(g2[:, t, :], hs[t][:].indirect(pos2_t[:]))
+            for u in range(2):
+                cols = slice(256 * u, 256 * (u + 1))
+                if b == 1:
+                    nc.vector.tensor_copy(g1[:, 3, cols], hs[3][:].indirect(pos1_t[:, 16 * u : 16 * (u + 1)]))
+                    nc.vector.tensor_copy(g2[:, 3, cols], hs[3][:].indirect(pos2_t[:, 16 * u : 16 * (u + 1)]))
+                nc.vector.tensor_tensor(woven(z[:, cols, :]), weave(g1[:, :, cols]), weave(g2[:, :, cols]), ALU.max)
+                zw = keep.tile([P, 256], U32, name=f"z_w{b}{u}", align_bytes=64)
+                zs = keep.tile([P, 256], U8, name=f"z_sc{b}{u}", align_bytes=64)
+                nc.vector.quantize_mx(
+                    out=zw[:].bitcast(FP8X4), scales=zs[:], in_=z[:, cols, :].rearrange("p m t -> p (m t)")
+                )
+                z_w[b, u], z_sc[b, u] = zw, zs
+
+        ys = [keep.tile([P, P1], F32, name=f"y{j}") for j in range(4)]
+        for u in range(2):
+            for j in range(4):
+                acc = psum.tile([P, 256], F32, name="acc")
+                for b in range(2):
+                    nc.tensor.matmul_mx(
+                        out=acc[:],
+                        lhsT=w2_w[b][:, P * j : P * (j + 1)].bitcast(FP8X4),
+                        lhsT_scale=w2_sc[b][:, P * j : P * (j + 1)],
+                        rhs=z_w[b, u][:].bitcast(FP8X4),
+                        rhs_scale=z_sc[b, u][:],
+                        start=(b == 0),
+                        stop=(b == 1),
+                    )
+                nc.scalar.copy(ys[j][:, 256 * u : 256 * (u + 1)], acc[:])
+
+        for j in range(4):
+            right = keep.tile([P, P2], F32, name=f"right{j}")
+            nc.vector.tensor_copy(right[:], ys[j][:].indirect(pos4_t[:]))
+            size = keep.tile([P, P2], F32, name=f"size{j}")
+            nc.scalar.activation(size[:], right[:], ACT.Abs)
+            root = keep.tile([P, P2], F32, name=f"root{j}")
+            nc.scalar.activation(root[:], size[:], ACT.Abs_reciprocal_sqrt, bias=1.0)
+            damp = keep.tile([P, P2], F32, name=f"damp{j}")
+            nc.scalar.activation(damp[:], root[:], ACT.Square)
+            res = keep.tile([P, P2], F32, name=f"res{j}")
+            nc.vector.tensor_tensor(res[:], ys[j][:].indirect(pos3_t[:]), damp[:], ALU.mult)
+            nc.sync.dma_start(out[P * j : P * (j + 1), :], res[:])

@@ -34,55 +34,60 @@ def tile_list_rumour_cascade_scores_kernel(
             nc.sync.dma_start(lst[:], src)
             return lst
 
-        tab_sc = keep.tile([P, T], U8, name="tab_sc", align_bytes=64)
-        for q in range(4):
-            nc.vector.memset(tab_sc[32 * q : 32 * q + 24, :].bitcast(I32), 0)
         w1_sc_raw = keep.tile([P, 2 * H], U8, name="w1_sc_raw", align_bytes=64)
         nc.vector.memset(w1_sc_raw[:].bitcast(I32), 0)
-        v_sc = [keep.tile([P, S], U8, name=f"v_sc{a}", align_bytes=64) for a in range(2)]
-        for a in range(2):
-            nc.vector.memset(v_sc[a][96:128, :].bitcast(I32), 0)
+        tab_sc = keep.tile([P, T], U8, name="tab_sc", tag="stage0", align_bytes=64)
+        for q in range(4):
+            nc.vector.memset(tab_sc[32 * q : 32 * q + 24, :].bitcast(I32), 0)
+        gain_rows = keep.tile([P, P], F32, name="gain_rows")
+        for b in range(2):
+            nc.scalar.dma_start(
+                gain_rows[120 + 4 * b : 124 + 4 * b, :].rearrange("t (B i) -> t B i", i=8),
+                gain[HALF * b : HALF * (b + 1)].rearrange("(B t i) -> t B i", t=4, i=8),
+            )
+        nc.gpsimd.memset(gain_rows[0:96, :], 0.0)
+        nc.gpsimd.memset(gain_rows[96:120, :], 0.0)
 
         offs_t = load_list(offs, "offs_t")
         for q in range(4):
             nc.sync.dma_start(
                 tab_sc[32 * q + 24 : 32 * q + 32, :].bitcast(I32), tab_scales[:, 4 * q : 4 * q + 4, :].bitcast(I32)
             )
-        tab_w = [keep.tile([P, T], U32, name=f"tab_w{a}", align_bytes=64) for a in range(2)]
-        w1_raw = [keep.tile([P, 2 * H], U8, name=f"w1_raw{b}", align_bytes=64) for b in range(2)]
-        for a in range(2):
+        tab_w = [keep.tile([P, T], U32, name=f"tab_w{a}", tag=f"stage{a + 1}", align_bytes=64) for a in range(2)]
+        w1_raw = []
+
+        def load_table(a):
             nc.sync.dma_start(tab_w[a][:].bitcast(I32), tab_words[a].rearrange("p t i -> p (t i)").bitcast(I32))
+
+        def load_w1(b, tag):
+            raw = keep.tile([P, 2 * H], U8, name="w1_raw", tag=tag, align_bytes=64)
             nc.sync.dma_start(
-                w1_raw[a][:].bitcast(I32).rearrange("p (a c) -> p a c", a=2),
-                w1_words[:, :, H * a : H * (a + 1)].rearrange("a p c -> p a c").bitcast(I32),
+                raw[:].bitcast(I32).rearrange("p (a c) -> p a c", a=2),
+                w1_words[:, :, H * b : H * (b + 1)].rearrange("a p c -> p a c").bitcast(I32),
             )
+            w1_raw.append(raw)
+
+        load_table(0)
+        load_w1(0, "stage3")
         for q in range(4):
-            nc.scalar.dma_start(
+            nc.sync.dma_start(
                 w1_sc_raw[32 * q : 32 * q + 4, :].bitcast(I32).rearrange("p (a c) -> p a c", a=2),
                 w1_scales[:, 4 * q : 4 * q + 4, :].rearrange("a r c -> r a c").bitcast(I32),
             )
-        gain_rows = keep.tile([P, P], F32, name="gain_rows")
-        nc.gpsimd.memset(gain_rows[:], 0.0)
-        for b in range(2):
-            nc.gpsimd.dma_start(
-                gain_rows[4 * b : 4 * (b + 1), :].rearrange("t (B i) -> t B i", i=8),
-                gain[HALF * b : HALF * (b + 1)].rearrange("(B t i) -> t B i", t=4, i=8),
-            )
+        load_table(1)
         ident = keep.tile([P, P], F32, name="ident")
         make_identity(nc, ident[:])
         gain_cols = psum.tile([P, P], F32, name="acc")
         nc.tensor.transpose(gain_cols[:], gain_rows[:], ident[:])
         log_gain = keep.tile([P, 8], F32, name="log_gain")
-        nc.scalar.activation(log_gain[:], gain_cols[:, 0:8], ACT.Ln)
+        nc.scalar.activation(log_gain[:], gain_cols[:, 120:128], ACT.Ln)
+        v_sc = [keep.tile([P, S], U8, name=f"v_sc{a}", align_bytes=64) for a in range(2)]
+        for a in range(2):
+            nc.gpsimd.memset(v_sc[a][96:128, :].bitcast(I32), 0)
+        warm = keep.tile([P, 16], F32, name="warm")
+        nc.scalar.activation(warm[:, 0:1], log_gain[:, 0:1], ACT.Exp)
         pos1_t = load_list(pos1, "pos1_t")
         pos2_t = load_list(pos2, "pos2_t")
-        w2_raw = []
-        for b in range(2):
-            raw = keep.tile([P, 4, N], F32, name=f"w2_raw{b}")
-            rows = w2[HALF * b : HALF * (b + 1), :].rearrange("(B t i) n -> t B i n", t=4, i=8)
-            for t in range(4):
-                nc.sync.dma_start(raw[:, t, :], rows[t])
-            w2_raw.append(raw)
         pos3_t = load_list(pos3, "pos3_t")
         pos4_t = load_list(pos4, "pos4_t")
 
@@ -91,32 +96,57 @@ def tile_list_rumour_cascade_scores_kernel(
         for a in range(2):
             first = 24 + 4 * a
             nc.scalar.dma_start(v_sc[a][0:100, :].bitcast(I32), picked_sc[first : first + 100, :].bitcast(I32))
+        load_w1(1, "stage0")
         v_w0 = keep.tile([P, S], U32, name="v_w0", align_bytes=64)
         nc.vector.tensor_copy(v_w0[:], tab_w[0][:].indirect(offs_t[:]))
 
-        w1_w, w1_sc = [], []
+        w2_raw = []
 
-        def order_w1(b):
-            words = keep.tile([P, 2 * 4 * 256], U8, name=f"w1_w{b}", align_bytes=64)
+        def load_w2(b, tag):
+            raw = keep.tile([P, 4, N], F32, name="w2_raw", tag=tag, align_bytes=64)
+            rows = w2[HALF * b : HALF * (b + 1), :].rearrange("(B t i) n -> t B i n", t=4, i=8)
+            for t in range(4):
+                nc.sync.dma_start(raw[:, t, :], rows[t])
+            w2_raw.append(raw)
+
+        load_w2(0, "stage1")
+
+        w1_w, w1_sc = {}, {}
+
+        def order_words(b, slots, tag):
+            count = slots.stop - slots.start
+            words = keep.tile([P, 2 * count * 256], U8, name="w1_w", tag=tag, align_bytes=64)
             nc.vector.tensor_copy(
-                words[:].bitcast(I32).rearrange("p (a t B i) -> p a t B i", a=2, t=4, i=4),
-                w1_raw[b][:].bitcast(I32).rearrange("p (a B t i) -> p a t B i", a=2, t=4, i=4),
+                words[:].bitcast(I32).rearrange("p (a t B i) -> p a t B i", a=2, t=count, i=4),
+                w1_raw[b][:].bitcast(I32).rearrange("p (a B t i) -> p a t B i", a=2, t=4, i=4)[:, :, slots],
             )
+            for a in range(2):
+                for n in range(count):
+                    j = count * a + n
+                    w1_w[a, b, slots.start + n] = words[:, 256 * j : 256 * (j + 1)]
+
+        def order_scales(b):
             sc = keep.tile([P, 2 * 4 * 128], U8, name=f"w1_sc{b}", align_bytes=64)
             nc.vector.tensor_copy(
                 sc[:].bitcast(I32).rearrange("p (a t B i) -> p a t B i", a=2, t=4, i=2),
                 w1_sc_raw[:].bitcast(I32).rearrange("p (a b B t i) -> p b a t B i", a=2, b=2, t=4, i=2)[:, b],
             )
-            w1_w.append(words)
-            w1_sc.append(sc)
+            for a in range(2):
+                for t in range(4):
+                    j = 4 * a + t
+                    w1_sc[a, b, t] = sc[:, 128 * j : 128 * (j + 1)]
 
-        order_w1(0)
+        order_words(0, slice(0, 1), "w1_first")
+        order_scales(0)
         v_w1 = []
         for u in range(2):
             vw = keep.tile([P, HALF], U32, name=f"v_w1_{u}", align_bytes=64)
             nc.vector.tensor_copy(vw[:], tab_w[1][:].indirect(offs_t[:, 32 * u : 32 * (u + 1)]))
             v_w1.append(vw)
-        order_w1(1)
+        order_words(0, slice(1, 4), "stage2")
+        load_w2(1, "stage3")
+        order_words(1, slice(0, 4), "w1_last")
+        order_scales(1)
 
         def moving(a, u):
             if a == 0:
@@ -131,11 +161,10 @@ def tile_list_rumour_cascade_scores_kernel(
                 cols = slice(HALF * u, HALF * (u + 1))
                 d = psum.tile([P, HALF], F32, name="acc")
                 for a in range(2):
-                    j = 4 * a + t
                     nc.tensor.matmul_mx(
                         out=d[:],
-                        lhsT=w1_w[b][:, 256 * j : 256 * (j + 1)].bitcast(FP4X4),
-                        lhsT_scale=w1_sc[b][:, 128 * j : 128 * (j + 1)],
+                        lhsT=w1_w[a, b, t].bitcast(FP4X4),
+                        lhsT_scale=w1_sc[a, b, t],
                         rhs=moving(a, u).bitcast(FP8X4),
                         rhs_scale=v_sc[a][:, cols],
                         start=(a == 0),
@@ -195,6 +224,7 @@ def tile_list_rumour_cascade_scores_kernel(
                 )
                 z_w[b, u], z_sc[b, u] = zw, zs
 
+        nc.scalar.activation(warm[:, 8:9], hs[3][:, 0:1], ACT.Abs_reciprocal_sqrt, bias=1.0)
         ys = [keep.tile([P, P1], F32, name=f"y{j}") for j in range(4)]
         for u in range(2):
             for j in range(4):

@@ -138,43 +138,44 @@ def tile_list_rumour_cascade_scores_kernel(
 
         order_words(0, slice(0, 1), "w1_first")
         order_scales(0)
-        v_w1 = []
-        for u in range(2):
-            vw = keep.tile([P, HALF], U32, name=f"v_w1_{u}", align_bytes=64)
-            nc.vector.tensor_copy(vw[:], tab_w[1][:].indirect(offs_t[:, 32 * u : 32 * (u + 1)]))
-            v_w1.append(vw)
+        v_w1 = keep.tile([P, S], U32, name="v_w1", align_bytes=64)
+        first_pieces = [slice(c, c + 256) for c in range(0, S, 256)]
+        for cols in first_pieces:
+            nc.vector.tensor_copy(v_w1[:, cols], tab_w[1][:].indirect(offs_t[:, cols.start // 16 : cols.stop // 16]))
+        v_w = [v_w0, v_w1]
         order_words(0, slice(1, 4), "stage2")
         load_w2(1, "stage3")
         order_words(1, slice(0, 4), "w1_last")
         order_scales(1)
 
-        def moving(a, u):
-            if a == 0:
-                return v_w0[:, HALF * u : HALF * (u + 1)]
-            return v_w1[u][:]
-
-        def responses(b, t):
-            h = keep.tile([P, S], F32, name=f"h{b}{t}")
-            sq = keep.tile([P, S], F32, name="sq", tag=f"scratch{4 * b + t}", align_bytes=64)
-            bias = log_gain[:, 4 * b + t : 4 * b + t + 1]
-            for u in range(2):
-                cols = slice(HALF * u, HALF * (u + 1))
-                d = psum.tile([P, HALF], F32, name="acc")
+        def responses(k, pieces):
+            b, t = divmod(k, 4)
+            h = keep.tile([P, S], F32, name=f"h{k}")
+            squares = []
+            for n, cols in enumerate(pieces):
+                width = cols.stop - cols.start
+                step = width if width == HALF else P
+                d = psum.tile([P, width], F32, name="acc")
                 for a in range(2):
-                    nc.tensor.matmul_mx(
-                        out=d[:],
-                        lhsT=w1_w[a, b, t].bitcast(FP4X4),
-                        lhsT_scale=w1_sc[a, b, t],
-                        rhs=moving(a, u).bitcast(FP8X4),
-                        rhs_scale=v_sc[a][:, cols],
-                        start=(a == 0),
-                        stop=(a == 1),
-                    )
-                nc.scalar.activation(sq[:, cols], d[:], ACT.Square)
-                if b == 0 and t == 0:
-                    nc.scalar.activation(h[:, cols], sq[:, cols], ACT.Exp, bias=bias, scale=-1.0)
-            if b or t:
-                nc.scalar.activation(h[:], sq[:], ACT.Exp, bias=bias, scale=-1.0)
+                    for c in range(0, width, step):
+                        part = slice(cols.start + c, cols.start + c + step)
+                        nc.tensor.matmul_mx(
+                            out=d[:, c : c + step],
+                            lhsT=w1_w[a, b, t].bitcast(FP4X4),
+                            lhsT_scale=w1_sc[a, b, t],
+                            rhs=v_w[a][:, part].bitcast(FP8X4),
+                            rhs_scale=v_sc[a][:, part],
+                            start=(a == 0 and c == 0),
+                            stop=(a == 1 and c + step == width),
+                        )
+                sq = keep.tile([P, width], F32, name="sq", tag=f"scratch{k}{n}", align_bytes=64)
+                nc.scalar.activation(sq[:], d[:], ACT.Square)
+                squares.append(sq)
+                if k == 0:
+                    nc.scalar.activation(h[:, cols], sq[:], ACT.Exp, bias=log_gain[:, k : k + 1], scale=-1.0)
+            if k:
+                for cols, sq in zip(pieces, squares):
+                    nc.scalar.activation(h[:, cols], sq[:], ACT.Exp, bias=log_gain[:, k : k + 1], scale=-1.0)
             return h
 
         def weave(ap3):
@@ -188,7 +189,7 @@ def tile_list_rumour_cascade_scores_kernel(
 
         def quantize_w2(b, cols, behind):
             width = cols.stop - cols.start
-            grouped = keep.tile([P, width, 4], BF16, name="w2_g", tag=f"scratch{behind}", align_bytes=64)
+            grouped = keep.tile([P, width, 4], BF16, name="w2_g", tag=behind, align_bytes=64)
             nc.scalar.copy(woven(grouped[:]), weave(w2_raw[b][:, :, cols]))
             nc.vector.quantize_mx(
                 out=w2_w[b][:, cols].bitcast(FP8X4),
@@ -196,35 +197,53 @@ def tile_list_rumour_cascade_scores_kernel(
                 in_=grouped[:].rearrange("p n t -> p (n t)"),
             )
 
-        w2_pieces = {3: (0, slice(0, 512)), 5: (1, slice(0, 256)), 7: (1, slice(256, 512))}
-        z_w, z_sc = {}, {}
-        for b in range(2):
-            g1 = keep.tile([P, 4, P1], F32, name=f"g1_{b}")
-            g2 = keep.tile([P, 4, P1], F32, name=f"g2_{b}")
-            z = keep.tile([P, P1, 4], BF16, name=f"z{b}", align_bytes=64)
-            hs = []
-            for t in range(4):
-                hs.append(responses(b, t))
-                if 4 * b + t in w2_pieces:
-                    quantize_w2(*w2_pieces[4 * b + t], 4 * b + t)
-                if b == 1 and t == 3:
-                    break
-                nc.vector.tensor_copy(g1[:, t, :], hs[t][:].indirect(pos1_t[:]))
-                nc.vector.tensor_copy(g2[:, t, :], hs[t][:].indirect(pos2_t[:]))
-            for u in range(2):
-                cols = slice(256 * u, 256 * (u + 1))
-                if b == 1:
-                    nc.vector.tensor_copy(g1[:, 3, cols], hs[3][:].indirect(pos1_t[:, 16 * u : 16 * (u + 1)]))
-                    nc.vector.tensor_copy(g2[:, 3, cols], hs[3][:].indirect(pos2_t[:, 16 * u : 16 * (u + 1)]))
-                nc.vector.tensor_tensor(woven(z[:, cols, :]), weave(g1[:, :, cols]), weave(g2[:, :, cols]), ALU.max)
-                zw = keep.tile([P, 256], U32, name=f"z_w{b}{u}", align_bytes=64)
-                zs = keep.tile([P, 256], U8, name=f"z_sc{b}{u}", align_bytes=64)
-                nc.vector.quantize_mx(
-                    out=zw[:].bitcast(FP8X4), scales=zs[:], in_=z[:, cols, :].rearrange("p m t -> p (m t)")
-                )
-                z_w[b, u], z_sc[b, u] = zw, zs
+        halves = [slice(0, HALF), slice(HALF, S)]
+        sharer = [keep.tile([P, 4, P1], F32, name=f"sharer{b}") for b in range(2)]
+        receiver = [keep.tile([P, 4, P1], F32, name=f"receiver{b}") for b in range(2)]
+        z_w = [keep.tile([P, P1], U32, name=f"z_w{b}", align_bytes=64) for b in range(2)]
+        z_sc = [keep.tile([P, P1], U8, name=f"z_sc{b}", align_bytes=64) for b in range(2)]
 
-        nc.scalar.activation(warm[:, 8:9], hs[3][:, 0:1], ACT.Abs_reciprocal_sqrt, bias=1.0)
+        def pick(dst, h, k, lst, cols):
+            nc.vector.tensor_copy(dst[k // 4][:, k % 4, cols], h[:].indirect(lst[:, cols.start // 16 : cols.stop // 16]))
+
+        def larger(b, cols, tag):
+            z = keep.tile([P, cols.stop - cols.start, 4], BF16, name="z", tag=tag, align_bytes=64)
+            nc.vector.tensor_tensor(woven(z[:]), weave(sharer[b][:, :, cols]), weave(receiver[b][:, :, cols]), ALU.max)
+            return z
+
+        def quantize_z(b, cols, z):
+            nc.vector.quantize_mx(
+                out=z_w[b][:, cols].bitcast(FP8X4), scales=z_sc[b][:, cols], in_=z[:].rearrange("p m t -> p (m t)")
+            )
+
+        every = slice(0, P1)
+        left, right = slice(0, 256), slice(256, 512)
+        all_h = []
+        for k in range(8):
+            h = responses(k, first_pieces if k == 0 else halves)
+            all_h.append(h)
+            if k == 7:
+                break
+            pick(sharer, h, k, pos1_t, every)
+            if k == 4:
+                z0 = larger(0, every, "scratch41")
+            pick(receiver, h, k, pos2_t, every)
+            if k == 4:
+                quantize_z(0, every, z0)
+                quantize_w2(0, every, "scratch40")
+            if k == 5:
+                quantize_w2(1, left, "scratch50")
+        pick(sharer, h, 7, pos1_t, left)
+        pick(receiver, h, 7, pos2_t, left)
+        pick(sharer, h, 7, pos1_t, right)
+        z_left = larger(1, left, "z_left")
+        pick(receiver, h, 7, pos2_t, right)
+        quantize_z(1, left, z_left)
+        z_right = larger(1, right, "z_right")
+        quantize_w2(1, right, "scratch70")
+        quantize_z(1, right, z_right)
+
+        nc.scalar.activation(warm[:, 8:9], h[:, 1023:1024], ACT.Abs_reciprocal_sqrt, bias=1.0)
         ys = [keep.tile([P, P1], F32, name=f"y{j}") for j in range(4)]
         for u in range(2):
             for j in range(4):
@@ -234,18 +253,18 @@ def tile_list_rumour_cascade_scores_kernel(
                         out=acc[:],
                         lhsT=w2_w[b][:, P * j : P * (j + 1)].bitcast(FP8X4),
                         lhsT_scale=w2_sc[b][:, P * j : P * (j + 1)],
-                        rhs=z_w[b, u][:].bitcast(FP8X4),
-                        rhs_scale=z_sc[b, u][:],
+                        rhs=z_w[b][:, 256 * u : 256 * (u + 1)].bitcast(FP8X4),
+                        rhs_scale=z_sc[b][:, 256 * u : 256 * (u + 1)],
                         start=(b == 0),
                         stop=(b == 1),
                     )
                 nc.scalar.copy(ys[j][:, 256 * u : 256 * (u + 1)], acc[:])
 
         for j in range(4):
-            right = keep.tile([P, P2], F32, name=f"right{j}")
-            nc.vector.tensor_copy(right[:], ys[j][:].indirect(pos4_t[:]))
+            other = keep.tile([P, P2], F32, name=f"right{j}")
+            nc.vector.tensor_copy(other[:], ys[j][:].indirect(pos4_t[:]))
             size = keep.tile([P, P2], F32, name=f"size{j}")
-            nc.scalar.activation(size[:], right[:], ACT.Abs)
+            nc.scalar.activation(size[:], other[:], ACT.Abs)
             root = keep.tile([P, P2], F32, name=f"root{j}")
             nc.scalar.activation(root[:], size[:], ACT.Abs_reciprocal_sqrt, bias=1.0)
             damp = keep.tile([P, P2], F32, name=f"damp{j}")

@@ -68,13 +68,15 @@ def tile_list_rumour_cascade_scores_kernel(
             w1_raw.append(raw)
 
         load_table(0)
-        load_w1(0, "stage3")
         for q in range(4):
             nc.sync.dma_start(
                 w1_sc_raw[32 * q : 32 * q + 4, :].bitcast(I32).rearrange("p (a c) -> p a c", a=2),
                 w1_scales[:, 4 * q : 4 * q + 4, :].rearrange("a r c -> r a c").bitcast(I32),
             )
+        load_w1(0, "stage3")
         load_table(1)
+        warm = keep.tile([P, 24], F32, name="warm")
+        nc.scalar.activation(warm[0:96, 16:17], gain_rows[0:96, 0:1], ACT.Ln, bias=1.0)
         ident = keep.tile([P, P], F32, name="ident")
         make_identity(nc, ident[:])
         gain_cols = psum.tile([P, P], F32, name="acc")
@@ -84,7 +86,6 @@ def tile_list_rumour_cascade_scores_kernel(
         v_sc = [keep.tile([P, S], U8, name=f"v_sc{a}", align_bytes=64) for a in range(2)]
         for a in range(2):
             nc.gpsimd.memset(v_sc[a][96:128, :].bitcast(I32), 0)
-        warm = keep.tile([P, 16], F32, name="warm")
         nc.scalar.activation(warm[:, 0:1], log_gain[:, 0:1], ACT.Exp)
         pos1_t = load_list(pos1, "pos1_t")
         pos2_t = load_list(pos2, "pos2_t")
@@ -151,8 +152,9 @@ def tile_list_rumour_cascade_scores_kernel(
         def responses(k, pieces):
             b, t = divmod(k, 4)
             h = keep.tile([P, S], F32, name=f"h{k}")
-            squares = []
-            for n, cols in enumerate(pieces):
+            sq = keep.tile([P, S], F32, name="sq", tag=f"scratch{k}", align_bytes=64)
+            bias = log_gain[:, k : k + 1]
+            for cols in pieces:
                 width = cols.stop - cols.start
                 step = width if width == HALF else P
                 d = psum.tile([P, width], F32, name="acc")
@@ -168,14 +170,11 @@ def tile_list_rumour_cascade_scores_kernel(
                             start=(a == 0 and c == 0),
                             stop=(a == 1 and c + step == width),
                         )
-                sq = keep.tile([P, width], F32, name="sq", tag=f"scratch{k}{n}", align_bytes=64)
-                nc.scalar.activation(sq[:], d[:], ACT.Square)
-                squares.append(sq)
+                nc.scalar.activation(sq[:, cols], d[:], ACT.Square)
                 if k == 0:
-                    nc.scalar.activation(h[:, cols], sq[:], ACT.Exp, bias=log_gain[:, k : k + 1], scale=-1.0)
+                    nc.scalar.activation(h[:, cols], sq[:, cols], ACT.Exp, bias=bias, scale=-1.0)
             if k:
-                for cols, sq in zip(pieces, squares):
-                    nc.scalar.activation(h[:, cols], sq[:], ACT.Exp, bias=log_gain[:, k : k + 1], scale=-1.0)
+                nc.scalar.activation(h[:], sq[:], ACT.Exp, bias=bias, scale=-1.0)
             return h
 
         def weave(ap3):
@@ -187,14 +186,14 @@ def tile_list_rumour_cascade_scores_kernel(
         w2_w = [keep.tile([P, N], U32, name=f"w2_w{b}", align_bytes=64) for b in range(2)]
         w2_sc = [keep.tile([P, N], U8, name=f"w2_sc{b}", align_bytes=64) for b in range(2)]
 
-        def quantize_w2(b, cols, behind):
-            width = cols.stop - cols.start
-            grouped = keep.tile([P, width, 4], BF16, name="w2_g", tag=behind, align_bytes=64)
-            nc.scalar.copy(woven(grouped[:]), weave(w2_raw[b][:, :, cols]))
+        def round_w2(b, grouped, cols):
+            nc.scalar.copy(woven(grouped[:, cols, :]), weave(w2_raw[b][:, :, cols]))
+
+        def quantize_w2(b, grouped, cols):
             nc.vector.quantize_mx(
                 out=w2_w[b][:, cols].bitcast(FP8X4),
                 scales=w2_sc[b][:, cols],
-                in_=grouped[:].rearrange("p n t -> p (n t)"),
+                in_=grouped[:, cols, :].rearrange("p n t -> p (n t)"),
             )
 
         halves = [slice(0, HALF), slice(HALF, S)]
@@ -226,21 +225,26 @@ def tile_list_rumour_cascade_scores_kernel(
                 break
             pick(sharer, h, k, pos1_t, every)
             if k == 4:
-                z0 = larger(0, every, "scratch41")
+                z0 = larger(0, every, "scratch4")
             pick(receiver, h, k, pos2_t, every)
             if k == 4:
                 quantize_z(0, every, z0)
-                quantize_w2(0, every, "scratch40")
-            if k == 5:
-                quantize_w2(1, left, "scratch50")
+            if k == 6:
+                grouped0 = keep.tile([P, N, 4], BF16, name="w2_g0", tag="scratch6", align_bytes=64)
+                round_w2(0, grouped0, every)
+        grouped1 = keep.tile([P, N, 4], BF16, name="w2_g1", tag="scratch7", align_bytes=64)
+        round_w2(1, grouped1, left)
+        round_w2(1, grouped1, right)
+        quantize_w2(0, grouped0, every)
         pick(sharer, h, 7, pos1_t, left)
         pick(receiver, h, 7, pos2_t, left)
         pick(sharer, h, 7, pos1_t, right)
         z_left = larger(1, left, "z_left")
         pick(receiver, h, 7, pos2_t, right)
         quantize_z(1, left, z_left)
+        quantize_w2(1, grouped1, left)
         z_right = larger(1, right, "z_right")
-        quantize_w2(1, right, "scratch70")
+        quantize_w2(1, grouped1, right)
         quantize_z(1, right, z_right)
 
         nc.scalar.activation(warm[:, 8:9], h[:, 1023:1024], ACT.Abs_reciprocal_sqrt, bias=1.0)

@@ -27,24 +27,23 @@ def tile_list_rumour_cascade_scores_kernel(
     nc = tc.nc
     with ExitStack() as ctx:
         keep = ctx.enter_context(tc.tile_pool(name="keep", bufs=1))
-        psum = ctx.enter_context(tc.psum_pool(name="psum", bufs=8))
+        psum = ctx.enter_context(tc.psum_pool(name="psum", bufs=1))
 
         def load_list(src, name):
             lst = keep.tile([P, src.shape[1]], U16, name=name)
             nc.sync.dma_start(lst[:], src)
             return lst
 
-        w1_sc_raw = keep.tile([P, 2 * H], U8, name="w1_sc_raw", align_bytes=64)
-        nc.vector.memset(w1_sc_raw[:].bitcast(I32), 0)
+        def bank(index, shape):
+            return psum.tile(shape, F32, name="bank", tag=f"bank{index}")
+
+        w1_sc = keep.tile([P, 2 * H], U8, name="w1_sc", align_bytes=64)
+        nc.vector.memset(w1_sc[:].bitcast(I32), 0)
         tab_sc = keep.tile([P, T], U8, name="tab_sc", tag="stage0", align_bytes=64)
         for q in range(4):
             nc.vector.memset(tab_sc[32 * q : 32 * q + 24, :].bitcast(I32), 0)
         gain_rows = keep.tile([P, P], F32, name="gain_rows")
-        for b in range(2):
-            nc.scalar.dma_start(
-                gain_rows[120 + 4 * b : 124 + 4 * b, :].rearrange("t (B i) -> t B i", i=8),
-                gain[HALF * b : HALF * (b + 1)].rearrange("(B t i) -> t B i", t=4, i=8),
-            )
+        nc.scalar.dma_start(gain_rows[120:128, :], gain.rearrange("(k p) -> k p", p=P))
         nc.gpsimd.memset(gain_rows[0:96, :], 0.0)
         nc.gpsimd.memset(gain_rows[96:120, :], 0.0)
 
@@ -54,23 +53,23 @@ def tile_list_rumour_cascade_scores_kernel(
                 tab_sc[32 * q + 24 : 32 * q + 32, :].bitcast(I32), tab_scales[:, 4 * q : 4 * q + 4, :].bitcast(I32)
             )
         tab_w = [keep.tile([P, T], U32, name=f"tab_w{a}", tag=f"stage{a + 1}", align_bytes=64) for a in range(2)]
-        w1_raw = []
+        w1_w = []
 
         def load_table(a):
             nc.sync.dma_start(tab_w[a][:].bitcast(I32), tab_words[a].rearrange("p t i -> p (t i)").bitcast(I32))
 
         def load_w1(b, tag):
-            raw = keep.tile([P, 2 * H], U8, name="w1_raw", tag=tag, align_bytes=64)
+            raw = keep.tile([P, 2 * H], U8, name="w1_w", tag=tag, align_bytes=64)
             nc.sync.dma_start(
                 raw[:].bitcast(I32).rearrange("p (a c) -> p a c", a=2),
                 w1_words[:, :, H * b : H * (b + 1)].rearrange("a p c -> p a c").bitcast(I32),
             )
-            w1_raw.append(raw)
+            w1_w.append(raw)
 
         load_table(0)
         for q in range(4):
             nc.sync.dma_start(
-                w1_sc_raw[32 * q : 32 * q + 4, :].bitcast(I32).rearrange("p (a c) -> p a c", a=2),
+                w1_sc[32 * q : 32 * q + 4, :].bitcast(I32).rearrange("p (a c) -> p a c", a=2),
                 w1_scales[:, 4 * q : 4 * q + 4, :].rearrange("a r c -> r a c").bitcast(I32),
             )
         load_w1(0, "stage3")
@@ -79,7 +78,7 @@ def tile_list_rumour_cascade_scores_kernel(
         nc.scalar.activation(warm[0:96, 16:17], gain_rows[0:96, 0:1], ACT.Ln, bias=1.0)
         ident = keep.tile([P, P], F32, name="ident")
         make_identity(nc, ident[:])
-        gain_cols = psum.tile([P, P], F32, name="acc")
+        gain_cols = bank(4, [P, P])
         nc.tensor.transpose(gain_cols[:], gain_rows[:], ident[:])
         log_gain = keep.tile([P, 8], F32, name="log_gain")
         nc.scalar.activation(log_gain[:], gain_cols[:, 120:128], ACT.Ln)
@@ -105,77 +104,41 @@ def tile_list_rumour_cascade_scores_kernel(
 
         def load_w2(b, tag):
             raw = keep.tile([P, 4, N], F32, name="w2_raw", tag=tag, align_bytes=64)
-            rows = w2[HALF * b : HALF * (b + 1), :].rearrange("(B t i) n -> t B i n", t=4, i=8)
-            for t in range(4):
-                nc.sync.dma_start(raw[:, t, :], rows[t])
+            nc.sync.dma_start(raw[:], w2[HALF * b : HALF * (b + 1), :].rearrange("(p j) n -> p j n", j=4))
             w2_raw.append(raw)
 
         load_w2(0, "stage1")
-
-        w1_w, w1_sc = {}, {}
-
-        def order_words(b, slots, tag):
-            count = slots.stop - slots.start
-            words = keep.tile([P, 2 * count * 256], U8, name="w1_w", tag=tag, align_bytes=64)
-            nc.vector.tensor_copy(
-                words[:].bitcast(I32).rearrange("p (a t B i) -> p a t B i", a=2, t=count, i=4),
-                w1_raw[b][:].bitcast(I32).rearrange("p (a B t i) -> p a t B i", a=2, t=4, i=4)[:, :, slots],
-            )
-            for a in range(2):
-                for n in range(count):
-                    j = count * a + n
-                    w1_w[a, b, slots.start + n] = words[:, 256 * j : 256 * (j + 1)]
-
-        def order_scales(b):
-            sc = keep.tile([P, 2 * 4 * 128], U8, name=f"w1_sc{b}", align_bytes=64)
-            nc.vector.tensor_copy(
-                sc[:].bitcast(I32).rearrange("p (a t B i) -> p a t B i", a=2, t=4, i=2),
-                w1_sc_raw[:].bitcast(I32).rearrange("p (a b B t i) -> p b a t B i", a=2, b=2, t=4, i=2)[:, b],
-            )
-            for a in range(2):
-                for t in range(4):
-                    j = 4 * a + t
-                    w1_sc[a, b, t] = sc[:, 128 * j : 128 * (j + 1)]
-
-        order_words(0, slice(0, 1), "w1_first")
-        order_scales(0)
         v_w1 = keep.tile([P, S], U32, name="v_w1", align_bytes=64)
         first_pieces = [slice(c, c + 256) for c in range(0, S, 256)]
         for cols in first_pieces:
             nc.vector.tensor_copy(v_w1[:, cols], tab_w[1][:].indirect(offs_t[:, cols.start // 16 : cols.stop // 16]))
         v_w = [v_w0, v_w1]
-        order_words(0, slice(1, 4), "stage2")
-        load_w2(1, "stage3")
-        order_words(1, slice(0, 4), "w1_last")
-        order_scales(1)
+        load_w2(1, "stage2")
 
-        def responses(k, pieces):
+        d_banks = [0]
+
+        def squares(k, pieces):
             b, t = divmod(k, 4)
-            h = keep.tile([P, S], F32, name=f"h{k}")
-            sq = keep.tile([P, S], F32, name="sq", tag=f"scratch{k}", align_bytes=64)
-            bias = log_gain[:, k : k + 1]
+            sq = keep.tile([P, S], F32, name=f"sq{k}")
             for cols in pieces:
                 width = cols.stop - cols.start
                 step = width if width == HALF else P
-                d = psum.tile([P, width], F32, name="acc")
+                d = bank(d_banks[0] % 4, [P, width])
+                d_banks[0] = d_banks[0] + 1
                 for a in range(2):
                     for c in range(0, width, step):
                         part = slice(cols.start + c, cols.start + c + step)
                         nc.tensor.matmul_mx(
                             out=d[:, c : c + step],
-                            lhsT=w1_w[a, b, t].bitcast(FP4X4),
-                            lhsT_scale=w1_sc[a, b, t],
+                            lhsT=w1_w[b][:, H * a + 256 * t : H * a + 256 * (t + 1)].bitcast(FP4X4),
+                            lhsT_scale=w1_sc[:, H * a + P * k : H * a + P * (k + 1)],
                             rhs=v_w[a][:, part].bitcast(FP8X4),
                             rhs_scale=v_sc[a][:, part],
                             start=(a == 0 and c == 0),
                             stop=(a == 1 and c + step == width),
                         )
                 nc.scalar.activation(sq[:, cols], d[:], ACT.Square)
-                if k == 0:
-                    nc.scalar.activation(h[:, cols], sq[:, cols], ACT.Exp, bias=bias, scale=-1.0)
-            if k:
-                nc.scalar.activation(h[:], sq[:], ACT.Exp, bias=bias, scale=-1.0)
-            return h
+            return sq
 
         def weave(ap3):
             return ap3.rearrange("p t (c i) -> p c t i", i=4)
@@ -186,83 +149,160 @@ def tile_list_rumour_cascade_scores_kernel(
         w2_w = [keep.tile([P, N], U32, name=f"w2_w{b}", align_bytes=64) for b in range(2)]
         w2_sc = [keep.tile([P, N], U8, name=f"w2_sc{b}", align_bytes=64) for b in range(2)]
 
-        def round_w2(b, grouped, cols):
-            nc.scalar.copy(woven(grouped[:, cols, :]), weave(w2_raw[b][:, :, cols]))
+        def round_w2(b):
+            grouped = keep.tile([P, N, 4], BF16, name=f"w2_g{b}", align_bytes=64)
+            nc.scalar.copy(woven(grouped[:]), weave(w2_raw[b][:]))
+            return grouped
 
-        def quantize_w2(b, grouped, cols):
+        def quantize_w2(b, grouped):
             nc.vector.quantize_mx(
-                out=w2_w[b][:, cols].bitcast(FP8X4),
-                scales=w2_sc[b][:, cols],
-                in_=grouped[:, cols, :].rearrange("p n t -> p (n t)"),
+                out=w2_w[b][:].bitcast(FP8X4), scales=w2_sc[b][:], in_=grouped[:].rearrange("p n t -> p (n t)")
             )
 
         halves = [slice(0, HALF), slice(HALF, S)]
-        sharer = [keep.tile([P, 4, P1], F32, name=f"sharer{b}") for b in range(2)]
-        receiver = [keep.tile([P, 4, P1], F32, name=f"receiver{b}") for b in range(2)]
         z_w = [keep.tile([P, P1], U32, name=f"z_w{b}", align_bytes=64) for b in range(2)]
         z_sc = [keep.tile([P, P1], U8, name=f"z_sc{b}", align_bytes=64) for b in range(2)]
 
-        def pick(dst, h, k, lst, cols):
-            nc.vector.tensor_copy(dst[k // 4][:, k % 4, cols], h[:].indirect(lst[:, cols.start // 16 : cols.stop // 16]))
+        def piece(name, k, cols):
+            return keep.tile([P, cols.stop - cols.start], F32, name=f"{name}{k}_{cols.start}")
 
-        def larger(b, cols, tag):
-            z = keep.tile([P, cols.stop - cols.start, 4], BF16, name="z", tag=tag, align_bytes=64)
-            nc.vector.tensor_tensor(woven(z[:]), weave(sharer[b][:, :, cols]), weave(receiver[b][:, :, cols]), ALU.max)
-            return z
+        def picked(sq, lst, cols):
+            return sq[:].indirect(lst[:, cols.start // 16 : cols.stop // 16])
 
-        def quantize_z(b, cols, z):
-            nc.vector.quantize_mx(
-                out=z_w[b][:, cols].bitcast(FP8X4), scales=z_sc[b][:, cols], in_=z[:].rearrange("p m t -> p (m t)")
+        def add_turned(x, term, first):
+            blocks = x.shape[1]
+            for g in range(blocks):
+                nc.tensor.matmul(
+                    x[:, g, :],
+                    lhsT=term[:, P * g : P * (g + 1)],
+                    rhs=ident[:],
+                    is_transpose=True,
+                    start=(first and g == 0),
+                    stop=(not first and g == blocks - 1),
+                )
+
+        def bell(k, x, turned):
+            t = k % 4
+            nc.scalar.activation(
+                turned[:, :, :, 64 * t : 64 * (t + 1)].rearrange("m u g (q e) -> m u g q e", e=2),
+                x.rearrange("m g (q u e) -> m u g q e", u=2, e=2),
+                ACT.Exp,
+                scale=-1.0,
             )
 
-        every = slice(0, P1)
-        left, right = slice(0, 256), slice(256, 512)
-        all_h = []
-        for k in range(8):
-            h = responses(k, first_pieces if k == 0 else halves)
-            all_h.append(h)
-            if k == 7:
-                break
-            pick(sharer, h, k, pos1_t, every)
-            if k == 4:
-                z0 = larger(0, every, "scratch4")
-            pick(receiver, h, k, pos2_t, every)
-            if k == 4:
-                quantize_z(0, every, z0)
-            if k == 6:
-                grouped0 = keep.tile([P, N, 4], BF16, name="w2_g0", tag="scratch6", align_bytes=64)
-                round_w2(0, grouped0, every)
-        grouped1 = keep.tile([P, N, 4], BF16, name="w2_g1", tag="scratch7", align_bytes=64)
-        round_w2(1, grouped1, left)
-        round_w2(1, grouped1, right)
-        quantize_w2(0, grouped0, every)
-        pick(sharer, h, 7, pos1_t, left)
-        pick(receiver, h, 7, pos2_t, left)
-        pick(sharer, h, 7, pos1_t, right)
-        z_left = larger(1, left, "z_left")
-        pick(receiver, h, 7, pos2_t, right)
-        quantize_z(1, left, z_left)
-        quantize_w2(1, grouped1, left)
-        z_right = larger(1, right, "z_right")
-        quantize_w2(1, grouped1, right)
-        quantize_z(1, right, z_right)
+        owns, gaps, cuts = {}, {}, {}
 
-        nc.scalar.activation(warm[:, 8:9], h[:, 1023:1024], ACT.Abs_reciprocal_sqrt, bias=1.0)
+        def pick_own(k, cols):
+            owns[k, cols.start] = piece("own", k, cols)
+            nc.vector.tensor_copy(owns[k, cols.start][:], picked(sqs[k], pos1_t, cols))
+
+        def pick_gap(k, cols):
+            gaps[k, cols.start] = piece("gap", k, cols)
+            nc.vector.tensor_tensor(
+                gaps[k, cols.start][:], picked(sqs[k], pos2_t, cols), owns[k, cols.start][:], ALU.subtract
+            )
+
+        def clip(k, cols):
+            cuts[k, cols.start] = piece("cut", k, cols)
+            nc.vector.tensor_scalar(
+                cuts[k, cols.start][:], gaps[k, cols.start][:], 0.0, log_gain[:, k : k + 1], ALU.min, ALU.subtract
+            )
+
+        def respond(k, cols, turned, x_bank):
+            clip(k, cols)
+            x = bank(x_bank, [P, (cols.stop - cols.start) // P, P])
+            add_turned(x, owns[k, cols.start], True)
+            add_turned(x, cuts[k, cols.start], False)
+            bell(k, x[:], turned)
+
+        def turn_back(b, turned, cols, first_block, blocks, z_bank, copy):
+            words = turned[:].rearrange("m u g r -> m (u g r)").bitcast(F32).rearrange("m (u g w) -> m u g w", u=2, w=P)
+            back = bank(z_bank, [P, blocks, 2, P])
+            for g in range(blocks):
+                for u in range(2):
+                    nc.tensor.transpose(back[:, g, u, :], words[:, u, first_block + g, :], ident[:])
+            start = cols.start + P * first_block
+            z = keep.tile([P, blocks * P * 4], BF16, name=f"z{b}_{start}", align_bytes=64)
+            copy(z[:].bitcast(F32).rearrange("p (g m u) -> p g m u", u=2, m=P), back[:].rearrange("p g u m -> p g m u"))
+            part = slice(start, start + P * blocks)
+            nc.vector.quantize_mx(out=z_w[b][:, part].bitcast(FP8X4), scales=z_sc[b][:, part], in_=z[:])
+
+        def turned_tile(b, cols):
+            return keep.tile([P, 2, (cols.stop - cols.start) // P, 256], BF16, name=f"turned{b}_{cols.start}")
+
+        every = slice(0, P1)
+        early, late = slice(0, 384), slice(384, 512)
+        sqs = [squares(k, first_pieces if k == 0 else halves) for k in range(8)]
+        w2_grouped = [round_w2(b) for b in range(2)]
+        turned0 = turned_tile(0, every)
+        turned1 = turned_tile(1, early)
+        turned2 = turned_tile(1, late)
+
+        def first_cols(k):
+            return every if k < 4 else early
+
+        for k in range(8):
+            pick_own(k, first_cols(k))
+            if k:
+                respond(k - 1, first_cols(k - 1), turned0 if k <= 4 else turned1, 4 + (k - 1) % 2)
+            pick_gap(k, first_cols(k))
+            if k == 4:
+                turn_back(0, turned0, every, 0, 2, 6, nc.scalar.copy)
+                turn_back(0, turned0, every, 2, 2, 7, nc.scalar.copy)
+        pick_own(4, late)
+        respond(7, early, turned1, 5)
+        for k in range(5, 8):
+            pick_own(k, late)
+        turn_back(1, turned1, early, 0, 2, 6, nc.scalar.copy)
+        turn_back(1, turned1, early, 2, 1, 7, nc.scalar.copy)
+        pick_gap(4, late)
+        for k in range(5, 8):
+            pick_gap(k, late)
+            clip(k - 1, late)
+        three = bank(4, [P, 3, P])
+        for n, terms in enumerate((owns, cuts)):
+            for k in range(4, 7):
+                nc.tensor.matmul(
+                    three[:, k - 4, :],
+                    lhsT=terms[k, late.start][:],
+                    rhs=ident[:],
+                    is_transpose=True,
+                    start=(n == 0 and k == 4),
+                    stop=(n == 1 and k == 6),
+                )
+        nc.scalar.activation(
+            turned2[:, :, 0, 0:192].rearrange("m u (q e) -> m u q e", e=2),
+            three[:].rearrange("m t (q u e) -> m u (t q) e", u=2, e=2),
+            ACT.Exp,
+            scale=-1.0,
+        )
+        quantize_w2(0, w2_grouped[0])
+        respond(7, late, turned2, 5)
+        quantize_w2(1, w2_grouped[1])
+        turn_back(1, turned2, late, 0, 1, 6, nc.vector.tensor_copy)
+        nc.scalar.activation(warm[:, 8:9], turned2[:, 1, 0, 255:256], ACT.Abs_reciprocal_sqrt, bias=1.0)
+
+        accs = [bank(j, [P, P1]) for j in (5, 6, 4, 7)]
+
+        def second(j, b):
+            nc.tensor.matmul_mx(
+                out=accs[j][:],
+                lhsT=w2_w[b][:, P * j : P * (j + 1)].bitcast(FP8X4),
+                lhsT_scale=w2_sc[b][:, P * j : P * (j + 1)],
+                rhs=z_w[b][:].bitcast(FP8X4),
+                rhs_scale=z_sc[b][:],
+                start=(b == 0),
+                stop=(b == 1),
+            )
+
         ys = [keep.tile([P, P1], F32, name=f"y{j}") for j in range(4)]
-        for u in range(2):
-            for j in range(4):
-                acc = psum.tile([P, 256], F32, name="acc")
-                for b in range(2):
-                    nc.tensor.matmul_mx(
-                        out=acc[:],
-                        lhsT=w2_w[b][:, P * j : P * (j + 1)].bitcast(FP8X4),
-                        lhsT_scale=w2_sc[b][:, P * j : P * (j + 1)],
-                        rhs=z_w[b][:, 256 * u : 256 * (u + 1)].bitcast(FP8X4),
-                        rhs_scale=z_sc[b][:, 256 * u : 256 * (u + 1)],
-                        start=(b == 0),
-                        stop=(b == 1),
-                    )
-                nc.scalar.copy(ys[j][:, 256 * u : 256 * (u + 1)], acc[:])
+        for j in range(4):
+            second(j, 0)
+            second(j, 1)
+            if j == 0:
+                nc.vector.tensor_copy(ys[j][:], accs[j][:])
+            else:
+                nc.scalar.copy(ys[j][:], accs[j][:])
 
         for j in range(4):
             other = keep.tile([P, P2], F32, name=f"right{j}")

@@ -35,7 +35,7 @@ def tile_list_rumour_cascade_scores_kernel(
             return lst
 
         def bank(index, shape):
-            return psum.tile(shape, F32, name="bank", tag=f"bank{index}")
+            return psum.tile(shape, F32, name="bank", tag=f"bank{index}", offset=2048 * index)
 
         w1_sc = keep.tile([P, 2 * H], U8, name="w1_sc", align_bytes=64)
         nc.vector.memset(w1_sc[:].bitcast(I32), 0)
@@ -58,9 +58,8 @@ def tile_list_rumour_cascade_scores_kernel(
         def load_table(a):
             nc.sync.dma_start(tab_w[a][:].bitcast(I32), tab_words[a].rearrange("p t i -> p (t i)").bitcast(I32))
 
-        def load_w1(b, tag):
-            raw = keep.tile([P, 2 * H], U8, name="w1_w", tag=tag, align_bytes=64)
-            nc.sync.dma_start(
+        def load_w1(b, raw, queue):
+            queue.dma_start(
                 raw[:].bitcast(I32).rearrange("p (a c) -> p a c", a=2),
                 w1_words[:, :, H * b : H * (b + 1)].rearrange("a p c -> p a c").bitcast(I32),
             )
@@ -72,13 +71,13 @@ def tile_list_rumour_cascade_scores_kernel(
                 w1_sc[32 * q : 32 * q + 4, :].bitcast(I32).rearrange("p (a c) -> p a c", a=2),
                 w1_scales[:, 4 * q : 4 * q + 4, :].rearrange("a r c -> r a c").bitcast(I32),
             )
-        load_w1(0, "stage3")
+        load_w1(0, keep.tile([P, 2 * H], U8, name="w1_w0", align_bytes=64), nc.sync)
         load_table(1)
         warm = keep.tile([P, 24], F32, name="warm")
         nc.scalar.activation(warm[0:96, 16:17], gain_rows[0:96, 0:1], ACT.Ln, bias=1.0)
         ident = keep.tile([P, P], F32, name="ident")
         make_identity(nc, ident[:])
-        gain_cols = bank(4, [P, P])
+        gain_cols = bank(6, [P, P])
         nc.tensor.transpose(gain_cols[:], gain_rows[:], ident[:])
         log_gain = keep.tile([P, 8], F32, name="log_gain")
         nc.scalar.activation(log_gain[:], gain_cols[:, 120:128], ACT.Ln)
@@ -96,49 +95,54 @@ def tile_list_rumour_cascade_scores_kernel(
         for a in range(2):
             first = 24 + 4 * a
             nc.scalar.dma_start(v_sc[a][0:100, :].bitcast(I32), picked_sc[first : first + 100, :].bitcast(I32))
-        load_w1(1, "stage0")
-        v_w0 = keep.tile([P, S], U32, name="v_w0", align_bytes=64)
-        nc.vector.tensor_copy(v_w0[:], tab_w[0][:].indirect(offs_t[:]))
-
+        load_w1(1, keep.tile([P, 2 * H], U8, name="w1_w1", tag="stage0", align_bytes=64), nc.sync)
         w2_raw = []
 
-        def load_w2(b, tag):
-            raw = keep.tile([P, 4, N], F32, name="w2_raw", tag=tag, align_bytes=64)
+        def load_w2(b):
+            raw = keep.tile([P, 4, N], F32, name="w2_raw", tag=f"stage{b + 1}", align_bytes=64)
             nc.sync.dma_start(raw[:], w2[HALF * b : HALF * (b + 1), :].rearrange("(p j) n -> p j n", j=4))
             w2_raw.append(raw)
 
-        load_w2(0, "stage1")
-        v_w1 = keep.tile([P, S], U32, name="v_w1", align_bytes=64)
-        first_pieces = [slice(c, c + 256) for c in range(0, S, 256)]
-        for cols in first_pieces:
-            nc.vector.tensor_copy(v_w1[:, cols], tab_w[1][:].indirect(offs_t[:, cols.start // 16 : cols.stop // 16]))
-        v_w = [v_w0, v_w1]
-        load_w2(1, "stage2")
+        v_w = [keep.tile([P, S], U32, name=f"v_w{a}", align_bytes=64) for a in range(2)]
+
+        def pick_words(a, cols):
+            nc.vector.tensor_copy(v_w[a][:, cols], tab_w[a][:].indirect(offs_t[:, cols.start // 16 : cols.stop // 16]))
+
+        halves = [slice(0, HALF), slice(HALF, S)]
+        last_quarters = [slice(HALF, HALF + 256), slice(HALF + 256, S)]
+        pick_words(0, slice(0, S))
+        load_w2(0)
+        pick_words(1, halves[0])
+        for cols in last_quarters:
+            pick_words(1, cols)
+        load_w2(1)
 
         d_banks = [0]
 
-        def squares(k, pieces):
+        sqs = [keep.tile([P, 2 * S if k < 4 else S], F32, name=f"sq{k}") for k in range(8)]
+        for k in range(4):
+            nc.gpsimd.memset(sqs[k][:, S:], 0.0)
+
+        def square(k, cols):
             b, t = divmod(k, 4)
-            sq = keep.tile([P, S], F32, name=f"sq{k}")
-            for cols in pieces:
-                width = cols.stop - cols.start
-                step = width if width == HALF else P
-                d = bank(d_banks[0] % 4, [P, width])
-                d_banks[0] = d_banks[0] + 1
-                for a in range(2):
-                    for c in range(0, width, step):
-                        part = slice(cols.start + c, cols.start + c + step)
-                        nc.tensor.matmul_mx(
-                            out=d[:, c : c + step],
-                            lhsT=w1_w[b][:, H * a + 256 * t : H * a + 256 * (t + 1)].bitcast(FP4X4),
-                            lhsT_scale=w1_sc[:, H * a + P * k : H * a + P * (k + 1)],
-                            rhs=v_w[a][:, part].bitcast(FP8X4),
-                            rhs_scale=v_sc[a][:, part],
-                            start=(a == 0 and c == 0),
-                            stop=(a == 1 and c + step == width),
-                        )
-                nc.scalar.activation(sq[:, cols], d[:], ACT.Square)
-            return sq
+            width = cols.stop - cols.start
+            step = width if width == HALF else P
+            d = bank(d_banks[0] % 6, [P, width])
+            d_banks[0] = d_banks[0] + 1
+            order = (0, 1) if k == 0 else (1, 0)
+            for a in order:
+                for c in range(0, width, step):
+                    part = slice(cols.start + c, cols.start + c + step)
+                    nc.tensor.matmul_mx(
+                        out=d[:, c : c + step],
+                        lhsT=w1_w[b][:, H * a + 256 * t : H * a + 256 * (t + 1)].bitcast(FP4X4),
+                        lhsT_scale=w1_sc[:, H * a + P * k : H * a + P * (k + 1)],
+                        rhs=v_w[a][:, part].bitcast(FP8X4),
+                        rhs_scale=v_sc[a][:, part],
+                        start=(a == order[0] and c == 0),
+                        stop=(a == order[1] and c + step == width),
+                    )
+            nc.scalar.activation(sqs[k][:, cols], d[:], ACT.Square)
 
         def weave(ap3):
             return ap3.rearrange("p t (c i) -> p c t i", i=4)
@@ -146,25 +150,31 @@ def tile_list_rumour_cascade_scores_kernel(
         def woven(ap3):
             return ap3.rearrange("p (c i) t -> p c t i", i=4)
 
-        w2_w = [keep.tile([P, N], U32, name=f"w2_w{b}", align_bytes=64) for b in range(2)]
+        w2_w = {}
         w2_sc = [keep.tile([P, N], U8, name=f"w2_sc{b}", align_bytes=64) for b in range(2)]
 
-        def round_w2(b):
-            grouped = keep.tile([P, N, 4], BF16, name=f"w2_g{b}", align_bytes=64)
-            nc.scalar.copy(woven(grouped[:]), weave(w2_raw[b][:]))
-            return grouped
+        w2_grouped = [keep.tile([P, N, 4], BF16, name=f"w2_g{b}", align_bytes=64) for b in range(2)]
+
+        def round_w2_scalar(b, cols):
+            for c in range(cols.start, cols.stop, P):
+                nc.scalar.copy(woven(w2_grouped[b][:, c : c + P, :]), weave(w2_raw[b][:, :, c : c + P]))
+
+        def round_w2_pool(b, cols):
+            nc.gpsimd.tensor_scalar(
+                w2_grouped[b][:, cols, :], w2_raw[b][:, :, cols].rearrange("p j n -> p n j"), 1.0, 0.0, ALU.mult, ALU.add
+            )
 
         def quantize_w2(b, grouped):
+            w2_w[b] = keep.tile([P, N], U32, name="w2_w", tag=f"gap{6 + b}_{late.start}", align_bytes=64)
             nc.vector.quantize_mx(
                 out=w2_w[b][:].bitcast(FP8X4), scales=w2_sc[b][:], in_=grouped[:].rearrange("p n t -> p (n t)")
             )
 
-        halves = [slice(0, HALF), slice(HALF, S)]
         z_w = [keep.tile([P, P1], U32, name=f"z_w{b}", align_bytes=64) for b in range(2)]
         z_sc = [keep.tile([P, P1], U8, name=f"z_sc{b}", align_bytes=64) for b in range(2)]
 
         def piece(name, k, cols):
-            return keep.tile([P, cols.stop - cols.start], F32, name=f"{name}{k}_{cols.start}")
+            return keep.tile([P, cols.stop - cols.start], F32, name=f"{name}{k}_{cols.start}", align_bytes=64)
 
         def picked(sq, lst, cols):
             return sq[:].indirect(lst[:, cols.start // 16 : cols.stop // 16])
@@ -181,25 +191,32 @@ def tile_list_rumour_cascade_scores_kernel(
                     stop=(not first and g == blocks - 1),
                 )
 
-        def bell(k, x, turned):
+        def bell(k, x, turned, sign):
             t = k % 4
             nc.scalar.activation(
                 turned[:, :, :, 64 * t : 64 * (t + 1)].rearrange("m u g (q e) -> m u g q e", e=2),
                 x.rearrange("m g (q u e) -> m u g q e", u=2, e=2),
                 ACT.Exp,
-                scale=-1.0,
+                scale=sign,
             )
 
         owns, gaps, cuts = {}, {}, {}
 
         def pick_own(k, cols):
-            owns[k, cols.start] = piece("own", k, cols)
-            nc.vector.tensor_copy(owns[k, cols.start][:], picked(sqs[k], pos1_t, cols))
+            owns[k, cols.start] = piece("own", k, cols)[:]
+            if k < 4:
+                nc.vector.tensor_scalar(owns[k, cols.start], picked(sqs[k], pos1_t, cols), -1.0, 0.0, ALU.mult, ALU.add)
+            else:
+                nc.vector.tensor_copy(owns[k, cols.start], picked(sqs[k], pos1_t, cols))
+
+        def pick_late_own(k):
+            owns[k, late.start] = late_owns[:, k - 4, :]
+            nc.vector.tensor_copy(owns[k, late.start], picked(sqs[k], pos1_t, late))
 
         def pick_gap(k, cols):
             gaps[k, cols.start] = piece("gap", k, cols)
             nc.vector.tensor_tensor(
-                gaps[k, cols.start][:], picked(sqs[k], pos2_t, cols), owns[k, cols.start][:], ALU.subtract
+                gaps[k, cols.start][:], picked(sqs[k], pos2_t, cols), owns[k, cols.start], ALU.subtract
             )
 
         def clip(k, cols):
@@ -208,12 +225,35 @@ def tile_list_rumour_cascade_scores_kernel(
                 cuts[k, cols.start][:], gaps[k, cols.start][:], 0.0, log_gain[:, k : k + 1], ALU.min, ALU.subtract
             )
 
+        def share_out(k, cols):
+            key = (k, cols.start)
+            other = piece("other", k, cols)
+            gap = keep.tile([P, cols.stop - cols.start], F32, name="gap", tag=f"stage{k % 2 + 1}", align_bytes=64)
+            nc.vector.tensor_copy(other[:], picked(sqs[k], pos2_t, cols))
+            cuts[key] = piece("cut", k, cols)
+            if k < 4:
+                nc.gpsimd.tensor_tensor(gap[:], owns[key], other[:], ALU.add)
+                nc.scalar.activation(cuts[key][:], gap[:], ACT.Relu, scale=-1.0)
+            else:
+                nc.gpsimd.tensor_tensor(gap[:], owns[key], other[:], ALU.subtract)
+                nc.gpsimd.tensor_scalar(owns[key], owns[key], -1.0, log_gain[:, k : k + 1], ALU.mult, ALU.add)
+                nc.scalar.activation(cuts[key][:], gap[:], ACT.Relu)
+
         def respond(k, cols, turned, x_bank):
-            clip(k, cols)
             x = bank(x_bank, [P, (cols.stop - cols.start) // P, P])
             add_turned(x, owns[k, cols.start], True)
+            if k < 4:
+                for g in range(4):
+                    nc.tensor.matmul(
+                        x[:, g, :],
+                        lhsT=log_gain[:, k : k + 1].to_broadcast([P, P]),
+                        rhs=ident[:],
+                        is_transpose=True,
+                        start=False,
+                        stop=False,
+                    )
             add_turned(x, cuts[k, cols.start], False)
-            bell(k, x[:], turned)
+            bell(k, x[:], turned, 1.0)
 
         def turn_back(b, turned, cols, first_block, blocks, z_bank, copy):
             words = turned[:].rearrange("m u g r -> m (u g r)").bitcast(F32).rearrange("m (u g w) -> m u g w", u=2, w=P)
@@ -232,8 +272,16 @@ def tile_list_rumour_cascade_scores_kernel(
 
         every = slice(0, P1)
         early, late = slice(0, 384), slice(384, 512)
-        sqs = [squares(k, first_pieces if k == 0 else halves) for k in range(8)]
-        w2_grouped = [round_w2(b) for b in range(2)]
+        d_banks[0] = 1
+        for k in range(1):
+            square(k, halves[0])
+        for cols in last_quarters:
+            square(0, cols)
+        for k in range(1, 8):
+            for cols in halves:
+                square(k, cols)
+        round_w2_pool(0, every)
+        round_w2_pool(1, every)
         turned0 = turned_tile(0, every)
         turned1 = turned_tile(1, early)
         turned2 = turned_tile(1, late)
@@ -241,30 +289,43 @@ def tile_list_rumour_cascade_scores_kernel(
         def first_cols(k):
             return every if k < 4 else early
 
-        for k in range(8):
+        for k in range(6):
             pick_own(k, first_cols(k))
-            if k:
-                respond(k - 1, first_cols(k - 1), turned0 if k <= 4 else turned1, 4 + (k - 1) % 2)
-            pick_gap(k, first_cols(k))
-            if k == 4:
+            share_out(k, first_cols(k))
+            respond(k, first_cols(k), turned0 if k < 4 else turned1, (0, 1, 2, 5)[k % 4])
+            if k == 3:
                 turn_back(0, turned0, every, 0, 2, 6, nc.scalar.copy)
                 turn_back(0, turned0, every, 2, 2, 7, nc.scalar.copy)
-        pick_own(4, late)
-        respond(7, early, turned1, 5)
+        pick_own(6, early)
+        pick_own(7, early)
+        pick_gap(6, early)
+        pick_gap(7, early)
+        clip(6, early)
+        x6 = bank(2, [P, 3, P])
+        add_turned(x6, owns[6, early.start], True)
+        add_turned(x6, cuts[6, early.start], False)
+        bell(6, x6[:], turned1, -1.0)
+        late_owns = keep.tile([P, 4, P], F32, name="late_owns", tag="own3_0", align_bytes=64)
+        pick_late_own(4)
+        clip(7, early)
+        pair = psum.tile([P, 2, 4, P], F32, name="pair", offset=2048 * 4)
+        add_turned(pair[:, 0, 0:3, :], owns[7, early.start], True)
+        add_turned(pair[:, 0, 0:3, :], cuts[7, early.start], False)
+        bell(7, pair[:, 0, 0:3, :], turned1, -1.0)
         for k in range(5, 8):
-            pick_own(k, late)
+            pick_late_own(k)
         turn_back(1, turned1, early, 0, 2, 6, nc.scalar.copy)
         turn_back(1, turned1, early, 2, 1, 7, nc.scalar.copy)
         pick_gap(4, late)
         for k in range(5, 8):
             pick_gap(k, late)
             clip(k - 1, late)
-        three = bank(4, [P, 3, P])
+        three = bank(5, [P, 3, P])
         for n, terms in enumerate((owns, cuts)):
             for k in range(4, 7):
                 nc.tensor.matmul(
                     three[:, k - 4, :],
-                    lhsT=terms[k, late.start][:],
+                    lhsT=terms[k, late.start][:, :],
                     rhs=ident[:],
                     is_transpose=True,
                     start=(n == 0 and k == 4),
@@ -277,12 +338,16 @@ def tile_list_rumour_cascade_scores_kernel(
             scale=-1.0,
         )
         quantize_w2(0, w2_grouped[0])
-        respond(7, late, turned2, 5)
+        clip(7, late)
+        wide = psum.tile([P, 4, 4, P], F32, name="wide", offset=2048)
+        add_turned(wide[:, 3, 0:1, :], owns[7, late.start], True)
+        add_turned(wide[:, 3, 0:1, :], cuts[7, late.start], False)
+        bell(7, wide[:, 3, 0:1, :], turned2, -1.0)
         quantize_w2(1, w2_grouped[1])
-        turn_back(1, turned2, late, 0, 1, 6, nc.vector.tensor_copy)
+        turn_back(1, turned2, late, 0, 1, 0, nc.vector.tensor_copy)
         nc.scalar.activation(warm[:, 8:9], turned2[:, 1, 0, 255:256], ACT.Abs_reciprocal_sqrt, bias=1.0)
 
-        accs = [bank(j, [P, P1]) for j in (5, 6, 4, 7)]
+        accs = [bank(j, [P, P1]) for j in range(1, 5)]
 
         def second(j, b):
             nc.tensor.matmul_mx(

@@ -119,9 +119,7 @@ def tile_list_rumour_cascade_scores_kernel(
 
         d_banks = [0]
 
-        sqs = [keep.tile([P, 2 * S if k < 4 else S], F32, name=f"sq{k}") for k in range(8)]
-        for k in range(4):
-            nc.gpsimd.memset(sqs[k][:, S:], 0.0)
+        sqs = [keep.tile([P, S], F32, name=f"sq{k}") for k in range(8)]
 
         def square(k, cols):
             b, t = divmod(k, 4)
@@ -204,56 +202,46 @@ def tile_list_rumour_cascade_scores_kernel(
 
         def pick_own(k, cols):
             owns[k, cols.start] = piece("own", k, cols)[:]
-            if k < 4:
-                nc.vector.tensor_scalar(owns[k, cols.start], picked(sqs[k], pos1_t, cols), -1.0, 0.0, ALU.mult, ALU.add)
-            else:
-                nc.vector.tensor_copy(owns[k, cols.start], picked(sqs[k], pos1_t, cols))
+            nc.vector.tensor_copy(owns[k, cols.start], picked(sqs[k], pos1_t, cols))
 
         def pick_late_own(k):
             owns[k, late.start] = late_owns[:, k - 4, :]
             nc.vector.tensor_copy(owns[k, late.start], picked(sqs[k], pos1_t, late))
 
         def pick_gap(k, cols):
-            gaps[k, cols.start] = piece("gap", k, cols)
+            gaps[k, cols.start] = early_gaps[:, k - 4, :] if cols.start == 0 else piece("gap", k, cols)[:]
             nc.vector.tensor_tensor(
-                gaps[k, cols.start][:], picked(sqs[k], pos2_t, cols), owns[k, cols.start], ALU.subtract
+                gaps[k, cols.start], picked(sqs[k], pos2_t, cols), owns[k, cols.start], ALU.subtract
             )
 
         def clip(k, cols):
             cuts[k, cols.start] = piece("cut", k, cols)
             nc.vector.tensor_scalar(
-                cuts[k, cols.start][:], gaps[k, cols.start][:], 0.0, log_gain[:, k : k + 1], ALU.min, ALU.subtract
+                cuts[k, cols.start][:], gaps[k, cols.start], 0.0, log_gain[:, k : k + 1], ALU.min, ALU.subtract
             )
 
-        def share_out(k, cols):
-            key = (k, cols.start)
-            other = piece("other", k, cols)
-            gap = keep.tile([P, cols.stop - cols.start], F32, name="gap", tag=f"stage{k % 2 + 1}", align_bytes=64)
-            nc.vector.tensor_copy(other[:], picked(sqs[k], pos2_t, cols))
-            cuts[key] = piece("cut", k, cols)
-            if k < 4:
-                nc.gpsimd.tensor_tensor(gap[:], owns[key], other[:], ALU.add)
-                nc.scalar.activation(cuts[key][:], gap[:], ACT.Relu, scale=-1.0)
-            else:
-                nc.gpsimd.tensor_tensor(gap[:], owns[key], other[:], ALU.subtract)
-                nc.gpsimd.tensor_scalar(owns[key], owns[key], -1.0, log_gain[:, k : k + 1], ALU.mult, ALU.add)
-                nc.scalar.activation(cuts[key][:], gap[:], ACT.Relu)
+        def respond_shared(k, x_bank):
+            own = piece("own", k, every)
+            nc.vector.tensor_copy(own[:], picked(sqs[k], pos1_t, every))
+            other = piece("other", k, every)
+            nc.vector.tensor_copy(other[:], picked(sqs[k], pos2_t, every))
+            base = piece("base", k, every)[:] if k == 0 else shared[:, 3 + k, :]
+            nc.gpsimd.tensor_scalar(base, own[:], -1.0, log_gain[:, k : k + 1], ALU.mult, ALU.add)
+            gap = shared[:, k, :]
+            nc.gpsimd.tensor_tensor(gap, own[:], other[:], ALU.subtract)
+            cut = piece("cut", k, every)
+            nc.scalar.activation(cut[:], gap, ACT.Relu)
+            x = bank(x_bank, [P, 4, P])
+            add_turned(x, base, True)
+            add_turned(x, cut, False)
+            bell(k, x[:], turned0, 1.0)
 
-        def respond(k, cols, turned, x_bank):
-            x = bank(x_bank, [P, (cols.stop - cols.start) // P, P])
-            add_turned(x, owns[k, cols.start], True)
-            if k < 4:
-                for g in range(4):
-                    nc.tensor.matmul(
-                        x[:, g, :],
-                        lhsT=log_gain[:, k : k + 1].to_broadcast([P, P]),
-                        rhs=ident[:],
-                        is_transpose=True,
-                        start=False,
-                        stop=False,
-                    )
-            add_turned(x, cuts[k, cols.start], False)
-            bell(k, x[:], turned, 1.0)
+        def respond(k, x_bank):
+            clip(k, early)
+            x = bank(x_bank, [P, 3, P])
+            add_turned(x, owns[k, early.start], True)
+            add_turned(x, cuts[k, early.start], False)
+            bell(k, x[:], turned1, -1.0)
 
         def turn_back(b, turned, cols, first_block, blocks, z_bank, copy):
             words = turned[:].rearrange("m u g r -> m (u g r)").bitcast(F32).rearrange("m (u g w) -> m u g w", u=2, w=P)
@@ -281,31 +269,24 @@ def tile_list_rumour_cascade_scores_kernel(
             for cols in halves:
                 square(k, cols)
         round_w2_pool(0, every)
-        round_w2_pool(1, every)
         turned0 = turned_tile(0, every)
         turned1 = turned_tile(1, early)
         turned2 = turned_tile(1, late)
 
-        def first_cols(k):
-            return every if k < 4 else early
-
-        for k in range(6):
-            pick_own(k, first_cols(k))
-            share_out(k, first_cols(k))
-            respond(k, first_cols(k), turned0 if k < 4 else turned1, (0, 1, 2, 5)[k % 4])
-            if k == 3:
-                turn_back(0, turned0, every, 0, 2, 6, nc.scalar.copy)
-                turn_back(0, turned0, every, 2, 2, 7, nc.scalar.copy)
-        pick_own(6, early)
-        pick_own(7, early)
-        pick_gap(6, early)
-        pick_gap(7, early)
-        clip(6, early)
-        x6 = bank(2, [P, 3, P])
-        add_turned(x6, owns[6, early.start], True)
-        add_turned(x6, cuts[6, early.start], False)
-        bell(6, x6[:], turned1, -1.0)
-        late_owns = keep.tile([P, 4, P], F32, name="late_owns", tag="own3_0", align_bytes=64)
+        shared = keep.tile([P, 7, P1], F32, name="shared", tag="stage1", align_bytes=64)
+        for k in range(4):
+            respond_shared(k, (0, 1, 2, 5)[k])
+        turn_back(0, turned0, every, 0, 2, 6, nc.scalar.copy)
+        turn_back(0, turned0, every, 2, 2, 7, nc.scalar.copy)
+        for k in range(4, 8):
+            pick_own(k, early)
+        early_gaps = keep.tile([P, 4, 384], F32, name="early_gaps", tag="other3_0", align_bytes=64)
+        pick_gap(4, early)
+        for k in range(5, 8):
+            pick_gap(k, early)
+            respond(k - 1, k - 5)
+        round_w2_scalar(1, every)
+        late_owns = keep.tile([P, 4, P], F32, name="late_owns", tag="stage1", align_bytes=64)
         pick_late_own(4)
         clip(7, early)
         pair = psum.tile([P, 2, 4, P], F32, name="pair", offset=2048 * 4)

@@ -3,8 +3,8 @@ from contextlib import ExitStack
 import concourse.mybir as mybir
 from concourse.masks import make_identity
 
-K, H, N, T, S, P1, P2 = 1024, 1024, 512, 2048, 1024, 512, 256
-FLOPS = 2 * K * H * S + 2 * H * N * P1
+K, H, N, T, S, SHARES, PAIRS = 1024, 1024, 512, 2048, 1024, 512, 256
+FLOPS = 2 * K * H * S + 2 * H * N * SHARES
 
 F32 = mybir.dt.float32
 BF16 = mybir.dt.bfloat16
@@ -18,7 +18,14 @@ ACT = mybir.ActivationFunctionType
 ALU = mybir.AluOpType
 
 P = 128
-HALF = 512
+PASS = 512
+BANK_COLS = 512
+BANK_BYTES = 2048
+ROW_TILES = H // P
+D_BANKS = 6
+
+EVERY = slice(0, SHARES)
+EARLY, LATE = slice(0, SHARES - P), slice(SHARES - P, SHARES)
 
 
 def tile_list_rumour_cascade_scores_kernel(
@@ -29,23 +36,26 @@ def tile_list_rumour_cascade_scores_kernel(
         keep = ctx.enter_context(tc.tile_pool(name="keep", bufs=1))
         psum = ctx.enter_context(tc.psum_pool(name="psum", bufs=1))
 
+        def bank(index, shape):
+            return psum.tile(shape, F32, name="bank", tag=f"bank{index}", offset=BANK_BYTES * index)
+
         def load_list(src, name):
             lst = keep.tile([P, src.shape[1]], U16, name=name)
             nc.sync.dma_start(lst[:], src)
             return lst
 
-        def bank(index, shape):
-            return psum.tile(shape, F32, name="bank", tag=f"bank{index}", offset=2048 * index)
+        def entries(lst, cols):
+            return lst[:, cols.start // 16 : cols.stop // 16]
 
         w1_sc = keep.tile([P, 2 * H], U8, name="w1_sc", align_bytes=64)
-        nc.vector.memset(w1_sc[:].bitcast(I32), 0)
+        nc.gpsimd.memset(w1_sc[:].bitcast(I32), 0)
         tab_sc = keep.tile([P, T], U8, name="tab_sc", tag="stage0", align_bytes=64)
         for q in range(4):
             nc.vector.memset(tab_sc[32 * q : 32 * q + 24, :].bitcast(I32), 0)
         gain_rows = keep.tile([P, P], F32, name="gain_rows")
-        nc.scalar.dma_start(gain_rows[120:128, :], gain.rearrange("(k p) -> k p", p=P))
+        nc.scalar.dma_start(gain_rows[P - ROW_TILES : P, :], gain.rearrange("(k p) -> k p", p=P))
         nc.gpsimd.memset(gain_rows[0:96, :], 0.0)
-        nc.gpsimd.memset(gain_rows[96:120, :], 0.0)
+        nc.gpsimd.memset(gain_rows[96 : P - ROW_TILES, :], 0.0)
 
         offs_t = load_list(offs, "offs_t")
         for q in range(4):
@@ -53,37 +63,34 @@ def tile_list_rumour_cascade_scores_kernel(
                 tab_sc[32 * q + 24 : 32 * q + 32, :].bitcast(I32), tab_scales[:, 4 * q : 4 * q + 4, :].bitcast(I32)
             )
         tab_w = [keep.tile([P, T], U32, name=f"tab_w{a}", tag=f"stage{a + 1}", align_bytes=64) for a in range(2)]
-        w1_w = []
-
-        def load_table(a):
+        for a in range(2):
             nc.sync.dma_start(tab_w[a][:].bitcast(I32), tab_words[a].rearrange("p t i -> p (t i)").bitcast(I32))
-
-        def load_w1(b, raw, queue):
-            queue.dma_start(
-                raw[:].bitcast(I32).rearrange("p (a c) -> p a c", a=2),
-                w1_words[:, :, H * b : H * (b + 1)].rearrange("a p c -> p a c").bitcast(I32),
-            )
-            w1_w.append(raw)
-
-        load_table(0)
         for q in range(4):
             nc.sync.dma_start(
                 w1_sc[32 * q : 32 * q + 4, :].bitcast(I32).rearrange("p (a c) -> p a c", a=2),
                 w1_scales[:, 4 * q : 4 * q + 4, :].rearrange("a r c -> r a c").bitcast(I32),
             )
-        load_w1(0, keep.tile([P, 2 * H], U8, name="w1_w0", align_bytes=64), nc.sync)
-        load_table(1)
+
+        def load_w1(b, tag):
+            words = keep.tile([P, 2 * H], U8, name="w1_w", tag=tag, align_bytes=64)
+            nc.sync.dma_start(
+                words[:].bitcast(I32).rearrange("p (a c) -> p a c", a=2),
+                w1_words[:, :, H * b : H * (b + 1)].rearrange("a p c -> p a c").bitcast(I32),
+            )
+            return words
+
+        w1_w = [load_w1(0, "w1_first")]
         warm = keep.tile([P, 24], F32, name="warm")
         nc.scalar.activation(warm[0:96, 16:17], gain_rows[0:96, 0:1], ACT.Ln, bias=1.0)
         ident = keep.tile([P, P], F32, name="ident")
         make_identity(nc, ident[:])
         gain_cols = bank(6, [P, P])
         nc.tensor.transpose(gain_cols[:], gain_rows[:], ident[:])
-        log_gain = keep.tile([P, 8], F32, name="log_gain")
-        nc.scalar.activation(log_gain[:], gain_cols[:, 120:128], ACT.Ln)
+        log_gain = keep.tile([P, ROW_TILES], F32, name="log_gain")
+        nc.scalar.activation(log_gain[:], gain_cols[:, P - ROW_TILES : P], ACT.Ln)
         v_sc = [keep.tile([P, S], U8, name=f"v_sc{a}", align_bytes=64) for a in range(2)]
         for a in range(2):
-            nc.gpsimd.memset(v_sc[a][96:128, :].bitcast(I32), 0)
+            nc.gpsimd.memset(v_sc[a][96:P, :].bitcast(I32), 0)
         nc.scalar.activation(warm[:, 0:1], log_gain[:, 0:1], ACT.Exp)
         pos1_t = load_list(pos1, "pos1_t")
         pos2_t = load_list(pos2, "pos2_t")
@@ -95,45 +102,40 @@ def tile_list_rumour_cascade_scores_kernel(
         for a in range(2):
             first = 24 + 4 * a
             nc.scalar.dma_start(v_sc[a][0:100, :].bitcast(I32), picked_sc[first : first + 100, :].bitcast(I32))
-        load_w1(1, keep.tile([P, 2 * H], U8, name="w1_w1", tag="stage0", align_bytes=64), nc.sync)
-        w2_raw = []
+        w1_w.append(load_w1(1, "stage0"))
 
         def load_w2(b):
             raw = keep.tile([P, 4, N], F32, name="w2_raw", tag=f"stage{b + 1}", align_bytes=64)
-            nc.sync.dma_start(raw[:], w2[HALF * b : HALF * (b + 1), :].rearrange("(p j) n -> p j n", j=4))
-            w2_raw.append(raw)
+            nc.sync.dma_start(raw[:], w2[PASS * b : PASS * (b + 1), :].rearrange("(p j) n -> p j n", j=4))
+            return raw
 
         v_w = [keep.tile([P, S], U32, name=f"v_w{a}", align_bytes=64) for a in range(2)]
 
         def pick_words(a, cols):
-            nc.vector.tensor_copy(v_w[a][:, cols], tab_w[a][:].indirect(offs_t[:, cols.start // 16 : cols.stop // 16]))
+            nc.vector.tensor_copy(v_w[a][:, cols], tab_w[a][:].indirect(entries(offs_t, cols)))
 
-        halves = [slice(0, HALF), slice(HALF, S)]
-        last_quarters = [slice(HALF, HALF + 256), slice(HALF + 256, S)]
+        halves = [slice(0, BANK_COLS), slice(BANK_COLS, S)]
+        first_pieces = [halves[0], slice(BANK_COLS, BANK_COLS + 256), slice(BANK_COLS + 256, S)]
         pick_words(0, slice(0, S))
-        load_w2(0)
-        pick_words(1, halves[0])
-        for cols in last_quarters:
+        w2_raw = [load_w2(0)]
+        for cols in first_pieces:
             pick_words(1, cols)
-        load_w2(1)
+        w2_raw.append(load_w2(1))
 
-        d_banks = [0]
+        sqs = [keep.tile([P, S], F32, name=f"sq{k}") for k in range(ROW_TILES)]
 
-        sqs = [keep.tile([P, S], F32, name=f"sq{k}") for k in range(8)]
-
-        def square(k, cols):
+        def square(k, cols, d_bank):
             b, t = divmod(k, 4)
             width = cols.stop - cols.start
-            step = width if width == HALF else P
-            d = bank(d_banks[0] % 6, [P, width])
-            d_banks[0] = d_banks[0] + 1
+            step = width if width == BANK_COLS else P
+            d = bank(d_bank, [P, width])
             order = (0, 1) if k == 0 else (1, 0)
             for a in order:
                 for c in range(0, width, step):
                     part = slice(cols.start + c, cols.start + c + step)
                     nc.tensor.matmul_mx(
                         out=d[:, c : c + step],
-                        lhsT=w1_w[b][:, H * a + 256 * t : H * a + 256 * (t + 1)].bitcast(FP4X4),
+                        lhsT=w1_w[b][:, H * a + 2 * P * t : H * a + 2 * P * (t + 1)].bitcast(FP4X4),
                         lhsT_scale=w1_sc[:, H * a + P * k : H * a + P * (k + 1)],
                         rhs=v_w[a][:, part].bitcast(FP8X4),
                         rhs_scale=v_sc[a][:, part],
@@ -142,52 +144,42 @@ def tile_list_rumour_cascade_scores_kernel(
                     )
             nc.scalar.activation(sqs[k][:, cols], d[:], ACT.Square)
 
-        def weave(ap3):
-            return ap3.rearrange("p t (c i) -> p c t i", i=4)
+        d_pieces = [(k, cols) for k in range(ROW_TILES) for cols in (first_pieces if k == 0 else halves)]
+        for n, (k, cols) in enumerate(d_pieces):
+            square(k, cols, (n + 1) % D_BANKS)
 
-        def woven(ap3):
-            return ap3.rearrange("p (c i) t -> p c t i", i=4)
-
+        w2_grouped = [keep.tile([P, N, 4], BF16, name=f"w2_g{b}", align_bytes=64) for b in range(2)]
         w2_w = {}
         w2_sc = [keep.tile([P, N], U8, name=f"w2_sc{b}", align_bytes=64) for b in range(2)]
 
-        w2_grouped = [keep.tile([P, N, 4], BF16, name=f"w2_g{b}", align_bytes=64) for b in range(2)]
-
-        def round_w2_scalar(b, cols):
-            for c in range(cols.start, cols.stop, P):
-                nc.scalar.copy(woven(w2_grouped[b][:, c : c + P, :]), weave(w2_raw[b][:, :, c : c + P]))
-
-        def round_w2_pool(b, cols):
-            nc.gpsimd.tensor_scalar(
-                w2_grouped[b][:, cols, :], w2_raw[b][:, :, cols].rearrange("p j n -> p n j"), 1.0, 0.0, ALU.mult, ALU.add
-            )
-
-        def quantize_w2(b, grouped):
-            w2_w[b] = keep.tile([P, N], U32, name="w2_w", tag=f"gap{6 + b}_{late.start}", align_bytes=64)
+        def quantize_w2(b, tag):
+            w2_w[b] = keep.tile([P, N], U32, name="w2_w", tag=tag, align_bytes=64)
             nc.vector.quantize_mx(
-                out=w2_w[b][:].bitcast(FP8X4), scales=w2_sc[b][:], in_=grouped[:].rearrange("p n t -> p (n t)")
+                out=w2_w[b][:].bitcast(FP8X4), scales=w2_sc[b][:], in_=w2_grouped[b][:].rearrange("p n t -> p (n t)")
             )
 
-        z_w = [keep.tile([P, P1], U32, name=f"z_w{b}", align_bytes=64) for b in range(2)]
-        z_sc = [keep.tile([P, P1], U8, name=f"z_sc{b}", align_bytes=64) for b in range(2)]
+        nc.gpsimd.tensor_scalar(w2_grouped[0][:], w2_raw[0][:].rearrange("p j n -> p n j"), 1.0, 0.0, ALU.mult, ALU.add)
+
+        z_w = [keep.tile([P, SHARES], U32, name=f"z_w{b}", align_bytes=64) for b in range(2)]
+        z_sc = [keep.tile([P, SHARES], U8, name=f"z_sc{b}", align_bytes=64) for b in range(2)]
 
         def piece(name, k, cols):
             return keep.tile([P, cols.stop - cols.start], F32, name=f"{name}{k}_{cols.start}", align_bytes=64)
 
-        def picked(sq, lst, cols):
-            return sq[:].indirect(lst[:, cols.start // 16 : cols.stop // 16])
+        def picked(k, lst, cols):
+            return sqs[k][:].indirect(entries(lst, cols))
 
-        def add_turned(x, term, first):
+        def turn(x, term, start, stop):
+            nc.tensor.matmul(x, lhsT=term, rhs=ident[:], is_transpose=True, start=start, stop=stop)
+
+        def add_turned(x, first_term, second_term):
             blocks = x.shape[1]
-            for g in range(blocks):
-                nc.tensor.matmul(
-                    x[:, g, :],
-                    lhsT=term[:, P * g : P * (g + 1)],
-                    rhs=ident[:],
-                    is_transpose=True,
-                    start=(first and g == 0),
-                    stop=(not first and g == blocks - 1),
-                )
+            for n, term in enumerate((first_term, second_term)):
+                for g in range(blocks):
+                    turn(x[:, g, :], term[:, P * g : P * (g + 1)], n == 0 and g == 0, n == 1 and g == blocks - 1)
+
+        def turned_tile(b, cols):
+            return keep.tile([P, 2, (cols.stop - cols.start) // P, 2 * P], BF16, name=f"turned{b}_{cols.start}")
 
         def bell(k, x, turned, sign):
             t = k % 4
@@ -197,51 +189,6 @@ def tile_list_rumour_cascade_scores_kernel(
                 ACT.Exp,
                 scale=sign,
             )
-
-        owns, gaps, cuts = {}, {}, {}
-
-        def pick_own(k, cols):
-            owns[k, cols.start] = piece("own", k, cols)[:]
-            nc.vector.tensor_copy(owns[k, cols.start], picked(sqs[k], pos1_t, cols))
-
-        def pick_late_own(k):
-            owns[k, late.start] = late_owns[:, k - 4, :]
-            nc.vector.tensor_copy(owns[k, late.start], picked(sqs[k], pos1_t, late))
-
-        def pick_gap(k, cols):
-            gaps[k, cols.start] = early_gaps[:, k - 4, :] if cols.start == 0 else piece("gap", k, cols)[:]
-            nc.vector.tensor_tensor(
-                gaps[k, cols.start], picked(sqs[k], pos2_t, cols), owns[k, cols.start], ALU.subtract
-            )
-
-        def clip(k, cols):
-            cuts[k, cols.start] = piece("cut", k, cols)
-            nc.vector.tensor_scalar(
-                cuts[k, cols.start][:], gaps[k, cols.start], 0.0, log_gain[:, k : k + 1], ALU.min, ALU.subtract
-            )
-
-        def respond_shared(k, x_bank):
-            own = piece("own", k, every)
-            nc.vector.tensor_copy(own[:], picked(sqs[k], pos1_t, every))
-            other = piece("other", k, every)
-            nc.vector.tensor_copy(other[:], picked(sqs[k], pos2_t, every))
-            base = piece("base", k, every)[:] if k == 0 else shared[:, 3 + k, :]
-            nc.gpsimd.tensor_scalar(base, own[:], -1.0, log_gain[:, k : k + 1], ALU.mult, ALU.add)
-            gap = shared[:, k, :]
-            nc.gpsimd.tensor_tensor(gap, own[:], other[:], ALU.subtract)
-            cut = piece("cut", k, every)
-            nc.scalar.activation(cut[:], gap, ACT.Relu)
-            x = bank(x_bank, [P, 4, P])
-            add_turned(x, base, True)
-            add_turned(x, cut, False)
-            bell(k, x[:], turned0, 1.0)
-
-        def respond(k, x_bank):
-            clip(k, early)
-            x = bank(x_bank, [P, 3, P])
-            add_turned(x, owns[k, early.start], True)
-            add_turned(x, cuts[k, early.start], False)
-            bell(k, x[:], turned1, -1.0)
 
         def turn_back(b, turned, cols, first_block, blocks, z_bank, copy):
             words = turned[:].rearrange("m u g r -> m (u g r)").bitcast(F32).rearrange("m (u g w) -> m u g w", u=2, w=P)
@@ -255,110 +202,118 @@ def tile_list_rumour_cascade_scores_kernel(
             part = slice(start, start + P * blocks)
             nc.vector.quantize_mx(out=z_w[b][:, part].bitcast(FP8X4), scales=z_sc[b][:, part], in_=z[:])
 
-        def turned_tile(b, cols):
-            return keep.tile([P, 2, (cols.stop - cols.start) // P, 256], BF16, name=f"turned{b}_{cols.start}")
+        turned_first = turned_tile(0, EVERY)
+        turned_early = turned_tile(1, EARLY)
+        turned_late = turned_tile(1, LATE)
 
-        every = slice(0, P1)
-        early, late = slice(0, 384), slice(384, 512)
-        d_banks[0] = 1
-        for k in range(1):
-            square(k, halves[0])
-        for cols in last_quarters:
-            square(0, cols)
-        for k in range(1, 8):
-            for cols in halves:
-                square(k, cols)
-        round_w2_pool(0, every)
-        turned0 = turned_tile(0, every)
-        turned1 = turned_tile(1, early)
-        turned2 = turned_tile(1, late)
+        pooled = keep.tile([P, 7, SHARES], F32, name="pooled", tag="stage1", align_bytes=64)
+        for k, x_bank in enumerate((0, 1, 2, 5)):
+            own = piece("own", k, EVERY)
+            nc.vector.tensor_copy(own[:], picked(k, pos1_t, EVERY))
+            other = piece("other", k, EVERY)
+            nc.vector.tensor_copy(other[:], picked(k, pos2_t, EVERY))
+            base = piece("base", k, EVERY)[:] if k == 0 else pooled[:, 3 + k, :]
+            nc.gpsimd.tensor_scalar(base, own[:], -1.0, log_gain[:, k : k + 1], ALU.mult, ALU.add)
+            nc.gpsimd.tensor_tensor(pooled[:, k, :], own[:], other[:], ALU.subtract)
+            excess = piece("excess", k, EVERY)
+            nc.scalar.activation(excess[:], pooled[:, k, :], ACT.Relu)
+            x = bank(x_bank, [P, 4, P])
+            add_turned(x, base, excess)
+            bell(k, x[:], turned_first, 1.0)
+        for n in range(2):
+            turn_back(0, turned_first, EVERY, 2 * n, 2, 6 + n, nc.scalar.copy)
 
-        shared = keep.tile([P, 7, P1], F32, name="shared", tag="stage1", align_bytes=64)
-        for k in range(4):
-            respond_shared(k, (0, 1, 2, 5)[k])
-        turn_back(0, turned0, every, 0, 2, 6, nc.scalar.copy)
-        turn_back(0, turned0, every, 2, 2, 7, nc.scalar.copy)
+        owns, gaps, cuts = {}, {}, {}
+
+        def pick_own(k, cols, dst):
+            owns[k, cols.start] = dst
+            nc.vector.tensor_copy(dst, picked(k, pos1_t, cols))
+
+        def pick_gap(k, cols, dst):
+            gaps[k, cols.start] = dst
+            nc.vector.tensor_tensor(dst, picked(k, pos2_t, cols), owns[k, cols.start], ALU.subtract)
+
+        def clip(k, cols):
+            cuts[k, cols.start] = piece("cut", k, cols)[:]
+            nc.vector.tensor_scalar(
+                cuts[k, cols.start], gaps[k, cols.start], 0.0, log_gain[:, k : k + 1], ALU.min, ALU.subtract
+            )
+
+        def respond(k, cols, x, turned):
+            add_turned(x, owns[k, cols.start], cuts[k, cols.start])
+            bell(k, x, turned, -1.0)
+
+        early_blocks = EARLY.stop // P
         for k in range(4, 8):
-            pick_own(k, early)
-        early_gaps = keep.tile([P, 4, 384], F32, name="early_gaps", tag="other3_0", align_bytes=64)
-        pick_gap(4, early)
+            pick_own(k, EARLY, piece("own", k, EARLY)[:])
+        early_gaps = keep.tile([P, 4, EARLY.stop], F32, name="early_gaps", tag="other3_0", align_bytes=64)
+        pick_gap(4, EARLY, early_gaps[:, 0, :])
         for k in range(5, 8):
-            pick_gap(k, early)
-            respond(k - 1, k - 5)
-        round_w2_scalar(1, every)
+            pick_gap(k, EARLY, early_gaps[:, k - 4, :])
+            clip(k - 1, EARLY)
+            respond(k - 1, EARLY, bank(k - 5, [P, early_blocks, P])[:], turned_early)
+        for c in range(0, N, P):
+            nc.scalar.copy(
+                w2_grouped[1][:, c : c + P, :].rearrange("p (c i) t -> p c t i", i=4),
+                w2_raw[1][:, :, c : c + P].rearrange("p t (c i) -> p c t i", i=4),
+            )
         late_owns = keep.tile([P, 4, P], F32, name="late_owns", tag="stage1", align_bytes=64)
-        pick_late_own(4)
-        clip(7, early)
-        pair = psum.tile([P, 2, 4, P], F32, name="pair", offset=2048 * 4)
-        add_turned(pair[:, 0, 0:3, :], owns[7, early.start], True)
-        add_turned(pair[:, 0, 0:3, :], cuts[7, early.start], False)
-        bell(7, pair[:, 0, 0:3, :], turned1, -1.0)
+        pick_own(4, LATE, late_owns[:, 0, :])
+        clip(7, EARLY)
+        pair = psum.tile([P, 2, 4, P], F32, name="pair", offset=BANK_BYTES * 4)
+        respond(7, EARLY, pair[:, 0, 0:early_blocks, :], turned_early)
         for k in range(5, 8):
-            pick_late_own(k)
-        turn_back(1, turned1, early, 0, 2, 6, nc.scalar.copy)
-        turn_back(1, turned1, early, 2, 1, 7, nc.scalar.copy)
-        pick_gap(4, late)
+            pick_own(k, LATE, late_owns[:, k - 4, :])
+        turn_back(1, turned_early, EARLY, 0, 2, 6, nc.scalar.copy)
+        turn_back(1, turned_early, EARLY, 2, 1, 7, nc.scalar.copy)
+
+        pick_gap(4, LATE, piece("gap", 4, LATE)[:])
         for k in range(5, 8):
-            pick_gap(k, late)
-            clip(k - 1, late)
+            pick_gap(k, LATE, piece("gap", k, LATE)[:])
+            clip(k - 1, LATE)
         three = bank(5, [P, 3, P])
         for n, terms in enumerate((owns, cuts)):
             for k in range(4, 7):
-                nc.tensor.matmul(
-                    three[:, k - 4, :],
-                    lhsT=terms[k, late.start][:, :],
-                    rhs=ident[:],
-                    is_transpose=True,
-                    start=(n == 0 and k == 4),
-                    stop=(n == 1 and k == 6),
-                )
+                turn(three[:, k - 4, :], terms[k, LATE.start], n == 0 and k == 4, n == 1 and k == 6)
         nc.scalar.activation(
-            turned2[:, :, 0, 0:192].rearrange("m u (q e) -> m u q e", e=2),
+            turned_late[:, :, 0, 0 : 3 * 64].rearrange("m u (q e) -> m u q e", e=2),
             three[:].rearrange("m t (q u e) -> m u (t q) e", u=2, e=2),
             ACT.Exp,
             scale=-1.0,
         )
-        quantize_w2(0, w2_grouped[0])
-        clip(7, late)
-        wide = psum.tile([P, 4, 4, P], F32, name="wide", offset=2048)
-        add_turned(wide[:, 3, 0:1, :], owns[7, late.start], True)
-        add_turned(wide[:, 3, 0:1, :], cuts[7, late.start], False)
-        bell(7, wide[:, 3, 0:1, :], turned2, -1.0)
-        quantize_w2(1, w2_grouped[1])
-        turn_back(1, turned2, late, 0, 1, 0, nc.vector.tensor_copy)
-        nc.scalar.activation(warm[:, 8:9], turned2[:, 1, 0, 255:256], ACT.Abs_reciprocal_sqrt, bias=1.0)
+        quantize_w2(0, f"gap6_{LATE.start}")
+        clip(7, LATE)
+        wide = psum.tile([P, 4, 4, P], F32, name="wide", offset=BANK_BYTES)
+        respond(7, LATE, wide[:, 3, 0:1, :], turned_late)
+        quantize_w2(1, f"gap7_{LATE.start}")
+        turn_back(1, turned_late, LATE, 0, 1, 0, nc.vector.tensor_copy)
+        nc.scalar.activation(warm[:, 8:9], turned_late[:, 1, 0, 255:256], ACT.Abs_reciprocal_sqrt, bias=1.0)
 
-        accs = [bank(j, [P, P1]) for j in range(1, 5)]
+        accs = [bank(j + 1, [P, SHARES]) for j in range(N // P)]
+        ys = [keep.tile([P, SHARES], F32, name=f"y{j}") for j in range(N // P)]
+        for j in range(N // P):
+            for b in range(2):
+                nc.tensor.matmul_mx(
+                    out=accs[j][:],
+                    lhsT=w2_w[b][:, P * j : P * (j + 1)].bitcast(FP8X4),
+                    lhsT_scale=w2_sc[b][:, P * j : P * (j + 1)],
+                    rhs=z_w[b][:].bitcast(FP8X4),
+                    rhs_scale=z_sc[b][:],
+                    start=(b == 0),
+                    stop=(b == 1),
+                )
+            copy = nc.vector.tensor_copy if j == 0 else nc.scalar.copy
+            copy(ys[j][:], accs[j][:])
 
-        def second(j, b):
-            nc.tensor.matmul_mx(
-                out=accs[j][:],
-                lhsT=w2_w[b][:, P * j : P * (j + 1)].bitcast(FP8X4),
-                lhsT_scale=w2_sc[b][:, P * j : P * (j + 1)],
-                rhs=z_w[b][:].bitcast(FP8X4),
-                rhs_scale=z_sc[b][:],
-                start=(b == 0),
-                stop=(b == 1),
-            )
-
-        ys = [keep.tile([P, P1], F32, name=f"y{j}") for j in range(4)]
-        for j in range(4):
-            second(j, 0)
-            second(j, 1)
-            if j == 0:
-                nc.vector.tensor_copy(ys[j][:], accs[j][:])
-            else:
-                nc.scalar.copy(ys[j][:], accs[j][:])
-
-        for j in range(4):
-            other = keep.tile([P, P2], F32, name=f"right{j}")
-            nc.vector.tensor_copy(other[:], ys[j][:].indirect(pos4_t[:]))
-            size = keep.tile([P, P2], F32, name=f"size{j}")
-            nc.scalar.activation(size[:], other[:], ACT.Abs)
-            root = keep.tile([P, P2], F32, name=f"root{j}")
+        for j in range(N // P):
+            right = keep.tile([P, PAIRS], F32, name=f"right{j}")
+            nc.vector.tensor_copy(right[:], ys[j][:].indirect(pos4_t[:]))
+            size = keep.tile([P, PAIRS], F32, name=f"size{j}")
+            nc.scalar.activation(size[:], right[:], ACT.Abs)
+            root = keep.tile([P, PAIRS], F32, name=f"root{j}")
             nc.scalar.activation(root[:], size[:], ACT.Abs_reciprocal_sqrt, bias=1.0)
-            damp = keep.tile([P, P2], F32, name=f"damp{j}")
+            damp = keep.tile([P, PAIRS], F32, name=f"damp{j}")
             nc.scalar.activation(damp[:], root[:], ACT.Square)
-            res = keep.tile([P, P2], F32, name=f"res{j}")
+            res = keep.tile([P, PAIRS], F32, name=f"res{j}")
             nc.vector.tensor_tensor(res[:], ys[j][:].indirect(pos3_t[:]), damp[:], ALU.mult)
             nc.sync.dma_start(out[P * j : P * (j + 1), :], res[:])

@@ -50,26 +50,31 @@ def tile_list_rumour_cascade_scores_kernel(
         w1_sc = keep.tile([P, 2 * H], U8, name="w1_sc", align_bytes=64)
         nc.gpsimd.memset(w1_sc[:].bitcast(I32), 0)
         tab_sc = keep.tile([P, T], U8, name="tab_sc", tag="stage0", align_bytes=64)
-        for q in range(4):
-            nc.vector.memset(tab_sc[32 * q : 32 * q + 24, :].bitcast(I32), 0)
+        for first, last in ((0, 48), (64, 80), (96, P)):
+            nc.vector.memset(tab_sc[first:last, :].bitcast(I32), 0)
         gain_rows = keep.tile([P, P], F32, name="gain_rows")
         nc.scalar.dma_start(gain_rows[P - ROW_TILES : P, :], gain.rearrange("(k p) -> k p", p=P))
         nc.gpsimd.memset(gain_rows[0:96, :], 0.0)
         nc.gpsimd.memset(gain_rows[96 : P - ROW_TILES, :], 0.0)
 
         offs_t = load_list(offs, "offs_t")
-        for q in range(4):
-            nc.sync.dma_start(
-                tab_sc[32 * q + 24 : 32 * q + 32, :].bitcast(I32), tab_scales[:, 4 * q : 4 * q + 4, :].bitcast(I32)
-            )
+        scale_rows = tab_scales.rearrange("a (h u j) t -> u (a h) j t", h=2, u=2)
+        for u in range(2):
+            nc.sync.dma_start(tab_sc[48 + 32 * u : 64 + 32 * u, :].bitcast(I32), scale_rows[u].bitcast(I32))
         tab_w = [keep.tile([P, T], U32, name=f"tab_w{a}", tag=f"stage{a + 1}", align_bytes=64) for a in range(2)]
-        for a in range(2):
+
+        def load_table(a):
             nc.sync.dma_start(tab_w[a][:].bitcast(I32), tab_words[a].rearrange("p t i -> p (t i)").bitcast(I32))
-        for q in range(4):
+
+        def load_w1_scales(q):
             nc.sync.dma_start(
-                w1_sc[32 * q : 32 * q + 4, :].bitcast(I32).rearrange("p (a c) -> p a c", a=2),
+                w1_sc[32 * q : 32 * q + 4, :].bitcast(I32),
                 w1_scales[:, 4 * q : 4 * q + 4, :].rearrange("a r c -> r a c").bitcast(I32),
             )
+
+        load_w1_scales(0)
+        load_w1_scales(1)
+        load_table(0)
 
         def load_w1(b, tag):
             words = keep.tile([P, 2 * H], U8, name="w1_w", tag=tag, align_bytes=64)
@@ -79,7 +84,10 @@ def tile_list_rumour_cascade_scores_kernel(
             )
             return words
 
+        load_table(1)
         w1_w = [load_w1(0, "w1_first")]
+        load_w1_scales(2)
+        load_w1_scales(3)
         warm = keep.tile([P, 24], F32, name="warm")
         nc.scalar.activation(warm[0:96, 16:17], gain_rows[0:96, 0:1], ACT.Ln, bias=1.0)
         ident = keep.tile([P, P], F32, name="ident")
@@ -89,8 +97,6 @@ def tile_list_rumour_cascade_scores_kernel(
         log_gain = keep.tile([P, ROW_TILES], F32, name="log_gain")
         nc.scalar.activation(log_gain[:], gain_cols[:, P - ROW_TILES : P], ACT.Ln)
         v_sc = [keep.tile([P, S], U8, name=f"v_sc{a}", align_bytes=64) for a in range(2)]
-        for a in range(2):
-            nc.gpsimd.memset(v_sc[a][96:P, :].bitcast(I32), 0)
         nc.scalar.activation(warm[:, 0:1], log_gain[:, 0:1], ACT.Exp)
         pos1_t = load_list(pos1, "pos1_t")
         pos2_t = load_list(pos2, "pos2_t")
@@ -100,8 +106,11 @@ def tile_list_rumour_cascade_scores_kernel(
         picked_sc = keep.tile([P, S], U8, name="picked_sc", align_bytes=64)
         nc.vector.tensor_copy(picked_sc[:], tab_sc[:].indirect(offs_t[:]))
         for a in range(2):
-            first = 24 + 4 * a
-            nc.scalar.dma_start(v_sc[a][0:100, :].bitcast(I32), picked_sc[first : first + 100, :].bitcast(I32))
+            for h in range(2):
+                first = 48 + 4 * (2 * a + h)
+                nc.scalar.dma_start(
+                    v_sc[a][64 * h : 64 * (h + 1), :].bitcast(I32), picked_sc[first : first + 64, :].bitcast(I32)
+                )
         w1_w.append(load_w1(1, "stage0"))
 
         def load_w2(b):

@@ -24,6 +24,10 @@ BANK_BYTES = 2048
 ROW_TILES = H // P
 D_BANKS = 6
 
+TABLE_AT = (12288, 2048)
+W2_AT = (12288, 16384, 4096, 8192)
+LAST_GAP_AT = 33792
+
 EVERY = slice(0, SHARES)
 EARLY, LATE = slice(0, SHARES - P), slice(SHARES - P, SHARES)
 
@@ -34,10 +38,14 @@ def tile_list_rumour_cascade_scores_kernel(
     nc = tc.nc
     with ExitStack() as ctx:
         keep = ctx.enter_context(tc.tile_pool(name="keep", bufs=1))
+        stage = ctx.enter_context(tc.tile_pool(name="stage", bufs=1))
         psum = ctx.enter_context(tc.psum_pool(name="psum", bufs=1))
 
         def bank(index, shape):
             return psum.tile(shape, F32, name="bank", tag=f"bank{index}", offset=BANK_BYTES * index)
+
+        def placed(name, shape, dtype, at):
+            return stage.tile(shape, dtype, name=name, offset=at, align_bytes=64)
 
         def load_list(src, name):
             lst = keep.tile([P, src.shape[1]], U16, name=name)
@@ -49,7 +57,7 @@ def tile_list_rumour_cascade_scores_kernel(
 
         w1_sc = keep.tile([P, 2 * H], U8, name="w1_sc", align_bytes=64)
         nc.gpsimd.memset(w1_sc[:].bitcast(I32), 0)
-        tab_sc = keep.tile([P, T], U8, name="tab_sc", tag="stage0", align_bytes=64)
+        tab_sc = placed("tab_sc", [P, T], U8, 0)
         for first, last in ((0, 48), (64, 80), (96, P)):
             nc.vector.memset(tab_sc[first:last, :].bitcast(I32), 0)
         gain_rows = keep.tile([P, P], F32, name="gain_rows")
@@ -61,7 +69,7 @@ def tile_list_rumour_cascade_scores_kernel(
         scale_rows = tab_scales.rearrange("a (h u j) t -> u (a h) j t", h=2, u=2)
         for u in range(2):
             nc.sync.dma_start(tab_sc[48 + 32 * u : 64 + 32 * u, :].bitcast(I32), scale_rows[u].bitcast(I32))
-        tab_w = [keep.tile([P, T], U32, name=f"tab_w{a}", tag=f"stage{a + 1}", align_bytes=64) for a in range(2)]
+        tab_w = [placed(f"tab_w{a}", [P, T], U32, TABLE_AT[a]) for a in range(2)]
 
         def load_table(a):
             nc.sync.dma_start(tab_w[a][:].bitcast(I32), tab_words[a].rearrange("p t i -> p (t i)").bitcast(I32))
@@ -76,8 +84,7 @@ def tile_list_rumour_cascade_scores_kernel(
         load_w1_scales(1)
         load_table(0)
 
-        def load_w1(b, tag):
-            words = keep.tile([P, 2 * H], U8, name="w1_w", tag=tag, align_bytes=64)
+        def load_w1(b, words):
             nc.sync.dma_start(
                 words[:].bitcast(I32).rearrange("p (a c) -> p a c", a=2),
                 w1_words[:, :, H * b : H * (b + 1)].rearrange("a p c -> p a c").bitcast(I32),
@@ -85,7 +92,7 @@ def tile_list_rumour_cascade_scores_kernel(
             return words
 
         load_table(1)
-        w1_w = [load_w1(0, "w1_first")]
+        w1_w = [load_w1(0, keep.tile([P, 2 * H], U8, name="w1_first", align_bytes=64))]
         load_w1_scales(2)
         load_w1_scales(3)
         warm = keep.tile([P, 24], F32, name="warm")
@@ -98,24 +105,20 @@ def tile_list_rumour_cascade_scores_kernel(
         nc.scalar.activation(log_gain[:], gain_cols[:, P - ROW_TILES : P], ACT.Ln)
         v_sc = [keep.tile([P, S], U8, name=f"v_sc{a}", align_bytes=64) for a in range(2)]
         nc.scalar.activation(warm[:, 0:1], log_gain[:, 0:1], ACT.Exp)
-        pos1_t = load_list(pos1, "pos1_t")
-        pos2_t = load_list(pos2, "pos2_t")
-        pos3_t = load_list(pos3, "pos3_t")
-        pos4_t = load_list(pos4, "pos4_t")
 
         picked_sc = keep.tile([P, S], U8, name="picked_sc", align_bytes=64)
         nc.vector.tensor_copy(picked_sc[:], tab_sc[:].indirect(offs_t[:]))
         for a in range(2):
             for h in range(2):
                 first = 48 + 4 * (2 * a + h)
-                nc.scalar.dma_start(
+                nc.sync.dma_start(
                     v_sc[a][64 * h : 64 * (h + 1), :].bitcast(I32), picked_sc[first : first + 64, :].bitcast(I32)
                 )
-        w1_w.append(load_w1(1, "stage0"))
 
-        def load_w2(b):
-            raw = keep.tile([P, 4, N], F32, name="w2_raw", tag=f"stage{b + 1}", align_bytes=64)
-            nc.sync.dma_start(raw[:], w2[PASS * b : PASS * (b + 1), :].rearrange("(p j) n -> p j n", j=4))
+        def load_w2(n):
+            b, cols = n // 2, slice(N // 2 * (n % 2), N // 2 * (n % 2 + 1))
+            raw = placed(f"w2_raw{n}", [P, 4, N // 2], F32, W2_AT[n])
+            nc.sync.dma_start(raw[:], w2[PASS * b : PASS * (b + 1), cols].rearrange("(p j) n -> p j n", j=4))
             return raw
 
         v_w = [keep.tile([P, S], U32, name=f"v_w{a}", align_bytes=64) for a in range(2)]
@@ -126,10 +129,15 @@ def tile_list_rumour_cascade_scores_kernel(
         halves = [slice(0, BANK_COLS), slice(BANK_COLS, S)]
         first_pieces = [halves[0], slice(BANK_COLS, BANK_COLS + 256), slice(BANK_COLS + 256, S)]
         pick_words(0, slice(0, S))
-        w2_raw = [load_w2(0)]
+        pos1_t = load_list(pos1, "pos1_t")
+        pos2_t = load_list(pos2, "pos2_t")
+        w2_raw = [load_w2(0), load_w2(1)]
+        pos3_t = load_list(pos3, "pos3_t")
+        pos4_t = load_list(pos4, "pos4_t")
         for cols in first_pieces:
             pick_words(1, cols)
-        w2_raw.append(load_w2(1))
+        w1_w.append(load_w1(1, placed("w1_second", [P, 2 * H], U8, TABLE_AT[1])))
+        w2_raw.extend([load_w2(2), load_w2(3)])
 
         sqs = [keep.tile([P, S], F32, name=f"sq{k}") for k in range(ROW_TILES)]
 
@@ -158,19 +166,32 @@ def tile_list_rumour_cascade_scores_kernel(
             square(k, cols, (n + 1) % D_BANKS)
 
         w2_grouped = [keep.tile([P, N, 4], BF16, name=f"w2_g{b}", align_bytes=64) for b in range(2)]
-        w2_w = {}
-        w2_sc = [keep.tile([P, N], U8, name=f"w2_sc{b}", align_bytes=64) for b in range(2)]
+        w2_w = [keep.tile([P, N], U32, name=f"w2_w{b}", align_bytes=64) for b in range(2)]
+        w2_planes = {}
 
-        def quantize_w2(b, tag):
-            w2_w[b] = keep.tile([P, N], U32, name="w2_w", tag=tag, align_bytes=64)
-            nc.vector.quantize_mx(
-                out=w2_w[b][:].bitcast(FP8X4), scales=w2_sc[b][:], in_=w2_grouped[b][:].rearrange("p n t -> p (n t)")
+        def quantize_w2(half, planes):
+            w2_planes[half] = planes
+            cols = slice(N // 2 * half, N // 2 * (half + 1))
+            for b in range(2):
+                nc.vector.quantize_mx(
+                    out=w2_w[b][:, cols].bitcast(FP8X4),
+                    scales=planes[:, N // 2 * b : N // 2 * (b + 1)],
+                    in_=w2_grouped[b][:, cols, :].rearrange("p n t -> p (n t)"),
+                )
+
+        for n in range(2):
+            nc.gpsimd.tensor_scalar(
+                w2_grouped[0][:, N // 2 * n : N // 2 * (n + 1), :],
+                w2_raw[n][:].rearrange("p j n -> p n j"),
+                1.0,
+                0.0,
+                ALU.mult,
+                ALU.add,
             )
 
-        nc.gpsimd.tensor_scalar(w2_grouped[0][:], w2_raw[0][:].rearrange("p j n -> p n j"), 1.0, 0.0, ALU.mult, ALU.add)
-
         z_w = [keep.tile([P, SHARES], U32, name=f"z_w{b}", align_bytes=64) for b in range(2)]
-        z_sc = [keep.tile([P, SHARES], U8, name=f"z_sc{b}", align_bytes=64) for b in range(2)]
+        z_planes = placed("z_planes", [P, 2 * SHARES], U8, LAST_GAP_AT - 768)
+        z_sc = [z_planes[:, SHARES * b : SHARES * (b + 1)] for b in range(2)]
 
         def piece(name, k, cols):
             return keep.tile([P, cols.stop - cols.start], F32, name=f"{name}{k}_{cols.start}", align_bytes=64)
@@ -199,6 +220,10 @@ def tile_list_rumour_cascade_scores_kernel(
                 scale=sign,
             )
 
+        def quantize_z(b, z, start):
+            part = slice(start, start + z.shape[1] // 4)
+            nc.vector.quantize_mx(out=z_w[b][:, part].bitcast(FP8X4), scales=z_sc[b][:, part], in_=z[:])
+
         def turn_back(b, turned, cols, first_block, blocks, z_bank, copy):
             words = turned[:].rearrange("m u g r -> m (u g r)").bitcast(F32).rearrange("m (u g w) -> m u g w", u=2, w=P)
             back = bank(z_bank, [P, blocks, 2, P])
@@ -208,20 +233,19 @@ def tile_list_rumour_cascade_scores_kernel(
             start = cols.start + P * first_block
             z = keep.tile([P, blocks * P * 4], BF16, name=f"z{b}_{start}", align_bytes=64)
             copy(z[:].bitcast(F32).rearrange("p (g m u) -> p g m u", u=2, m=P), back[:].rearrange("p g u m -> p g m u"))
-            part = slice(start, start + P * blocks)
-            nc.vector.quantize_mx(out=z_w[b][:, part].bitcast(FP8X4), scales=z_sc[b][:, part], in_=z[:])
+            return b, z, start
 
         turned_first = turned_tile(0, EVERY)
         turned_early = turned_tile(1, EARLY)
         turned_late = turned_tile(1, LATE)
 
-        pooled = keep.tile([P, 7, SHARES], F32, name="pooled", tag="stage1", align_bytes=64)
+        pooled = placed("pooled", [P, 8, SHARES], F32, W2_AT[1])
         for k, x_bank in enumerate((0, 1, 2, 5)):
             own = piece("own", k, EVERY)
             nc.vector.tensor_copy(own[:], picked(k, pos1_t, EVERY))
             other = piece("other", k, EVERY)
             nc.vector.tensor_copy(other[:], picked(k, pos2_t, EVERY))
-            base = piece("base", k, EVERY)[:] if k == 0 else pooled[:, 3 + k, :]
+            base = pooled[:, 4 + k, :]
             nc.gpsimd.tensor_scalar(base, own[:], -1.0, log_gain[:, k : k + 1], ALU.mult, ALU.add)
             nc.gpsimd.tensor_tensor(pooled[:, k, :], own[:], other[:], ALU.subtract)
             excess = piece("excess", k, EVERY)
@@ -229,8 +253,7 @@ def tile_list_rumour_cascade_scores_kernel(
             x = bank(x_bank, [P, 4, P])
             add_turned(x, base, excess)
             bell(k, x[:], turned_first, 1.0)
-        for n in range(2):
-            turn_back(0, turned_first, EVERY, 2 * n, 2, 6 + n, nc.scalar.copy)
+        first_z = [turn_back(0, turned_first, EVERY, 2 * n, 2, 6 + n, nc.scalar.copy) for n in range(2)]
 
         owns, gaps, cuts = {}, {}, {}
 
@@ -264,21 +287,23 @@ def tile_list_rumour_cascade_scores_kernel(
         for c in range(0, N, P):
             nc.scalar.copy(
                 w2_grouped[1][:, c : c + P, :].rearrange("p (c i) t -> p c t i", i=4),
-                w2_raw[1][:, :, c : c + P].rearrange("p t (c i) -> p c t i", i=4),
+                w2_raw[2 + c // 256][:, :, c % 256 : c % 256 + P].rearrange("p t (c i) -> p c t i", i=4),
             )
-        late_owns = keep.tile([P, 4, P], F32, name="late_owns", tag="stage1", align_bytes=64)
+        late_owns = placed("late_owns", [P, 4, P], F32, W2_AT[1])
         pick_own(4, LATE, late_owns[:, 0, :])
         clip(7, EARLY)
         pair = psum.tile([P, 2, 4, P], F32, name="pair", offset=BANK_BYTES * 4)
         respond(7, EARLY, pair[:, 0, 0:early_blocks, :], turned_early)
         for k in range(5, 8):
             pick_own(k, LATE, late_owns[:, k - 4, :])
-        turn_back(1, turned_early, EARLY, 0, 2, 6, nc.scalar.copy)
-        turn_back(1, turned_early, EARLY, 2, 1, 7, nc.scalar.copy)
+        early_z = [
+            turn_back(1, turned_early, EARLY, 0, 2, 6, nc.scalar.copy),
+            turn_back(1, turned_early, EARLY, 2, 1, 7, nc.scalar.copy),
+        ]
 
         pick_gap(4, LATE, piece("gap", 4, LATE)[:])
         for k in range(5, 8):
-            pick_gap(k, LATE, piece("gap", k, LATE)[:])
+            pick_gap(k, LATE, (placed("last_gap", [P, P], F32, LAST_GAP_AT) if k == 7 else piece("gap", k, LATE))[:])
             clip(k - 1, LATE)
         three = bank(5, [P, 3, P])
         for n, terms in enumerate((owns, cuts)):
@@ -290,39 +315,58 @@ def tile_list_rumour_cascade_scores_kernel(
             ACT.Exp,
             scale=-1.0,
         )
-        quantize_w2(0, f"gap6_{LATE.start}")
         clip(7, LATE)
         wide = psum.tile([P, 4, 4, P], F32, name="wide", offset=BANK_BYTES)
         respond(7, LATE, wide[:, 3, 0:1, :], turned_late)
-        quantize_w2(1, f"gap7_{LATE.start}")
-        turn_back(1, turned_late, LATE, 0, 1, 0, nc.vector.tensor_copy)
-        nc.scalar.activation(warm[:, 8:9], turned_late[:, 1, 0, 255:256], ACT.Abs_reciprocal_sqrt, bias=1.0)
+        for made in first_z:
+            quantize_z(*made)
+        quantize_w2(0, placed("w2_planes", [P, N], U8, LAST_GAP_AT + 256))
+        quantize_z(*early_z[0])
+        late_z = turn_back(1, turned_late, LATE, 0, 1, 0, nc.scalar.copy)
+        quantize_z(*early_z[1])
+        quantize_z(*late_z)
+        warm_root = keep.tile([P, 8], F32, name="warm_root", tag=f"turned1_{LATE.start}")
+        nc.scalar.activation(warm_root[:, 0:1], log_gain[:, 0:1], ACT.Abs_reciprocal_sqrt, bias=1.0)
+
+        quantize_w2(1, keep.tile([P, N], U8, name="w2_right", tag=f"z1_{LATE.start}", align_bytes=64))
 
         accs = [bank(j + 1, [P, SHARES]) for j in range(N // P)]
-        ys = [keep.tile([P, SHARES], F32, name=f"y{j}") for j in range(N // P)]
+        ys, damps = {}, {}
         for j in range(N // P):
             for b in range(2):
                 nc.tensor.matmul_mx(
                     out=accs[j][:],
                     lhsT=w2_w[b][:, P * j : P * (j + 1)].bitcast(FP8X4),
-                    lhsT_scale=w2_sc[b][:, P * j : P * (j + 1)],
+                    lhsT_scale=w2_planes[j // 2][:, N // 2 * b + P * (j % 2) : N // 2 * b + P * (j % 2 + 1)],
                     rhs=z_w[b][:].bitcast(FP8X4),
-                    rhs_scale=z_sc[b][:],
+                    rhs_scale=z_sc[b],
                     start=(b == 0),
                     stop=(b == 1),
                 )
-            copy = nc.vector.tensor_copy if j == 0 else nc.scalar.copy
+
+        def leave(j, copy, tag):
+            ys[j] = keep.tile([P, SHARES], F32, name="y", tag=tag)
             copy(ys[j][:], accs[j][:])
 
-        for j in range(N // P):
-            right = keep.tile([P, PAIRS], F32, name=f"right{j}")
+        def damping(j):
+            right = keep.tile([P, PAIRS], F32, name="right", tag=f"right{j}")
             nc.vector.tensor_copy(right[:], ys[j][:].indirect(pos4_t[:]))
             size = keep.tile([P, PAIRS], F32, name=f"size{j}")
             nc.scalar.activation(size[:], right[:], ACT.Abs)
             root = keep.tile([P, PAIRS], F32, name=f"root{j}")
             nc.scalar.activation(root[:], size[:], ACT.Abs_reciprocal_sqrt, bias=1.0)
-            damp = keep.tile([P, PAIRS], F32, name=f"damp{j}")
-            nc.scalar.activation(damp[:], root[:], ACT.Square)
+            damps[j] = keep.tile([P, PAIRS], F32, name=f"damp{j}")
+            nc.scalar.activation(damps[j][:], root[:], ACT.Square)
+
+        leave(0, nc.vector.tensor_copy, "y0")
+        leave(1, nc.scalar.copy, "y1")
+        leave(2, nc.scalar.copy, "y2")
+        for j in range(2):
+            damping(j)
+        leave(3, nc.vector.tensor_copy, "right0")
+        for j in range(2, 4):
+            damping(j)
+        for j in range(N // P):
             res = keep.tile([P, PAIRS], F32, name=f"res{j}")
-            nc.vector.tensor_tensor(res[:], ys[j][:].indirect(pos3_t[:]), damp[:], ALU.mult)
+            nc.vector.tensor_tensor(res[:], ys[j][:].indirect(pos3_t[:]), damps[j][:], ALU.mult)
             nc.sync.dma_start(out[P * j : P * (j + 1), :], res[:])

@@ -24,9 +24,10 @@ BANK_BYTES = 2048
 ROW_TILES = H // P
 D_BANKS = 6
 
-TABLE_AT = (12288, 2048)
-W2_AT = (12288, 16384, 4096, 8192)
-LAST_GAP_AT = 33792
+TABLE_AT = (12352, 2112)
+W2_AT = (12352, 16448, 4160, 8256)
+LAST_GAP_AT = 43008
+POOL_TILES = 5
 
 EVERY = slice(0, SHARES)
 EARLY, LATE = slice(0, SHARES - P), slice(SHARES - P, SHARES)
@@ -57,7 +58,7 @@ def tile_list_rumour_cascade_scores_kernel(
 
         w1_sc = keep.tile([P, 2 * H], U8, name="w1_sc", align_bytes=64)
         nc.gpsimd.memset(w1_sc[:].bitcast(I32), 0)
-        tab_sc = placed("tab_sc", [P, T], U8, 0)
+        tab_sc = placed("tab_sc", [P, T + 4], U8, 0)
         for first, last in ((0, 48), (64, 80), (96, P)):
             nc.vector.memset(tab_sc[first:last, :].bitcast(I32), 0)
         gain_rows = keep.tile([P, P], F32, name="gain_rows")
@@ -68,7 +69,7 @@ def tile_list_rumour_cascade_scores_kernel(
         offs_t = load_list(offs, "offs_t")
         scale_rows = tab_scales.rearrange("a (h u j) t -> u (a h) j t", h=2, u=2)
         for u in range(2):
-            nc.sync.dma_start(tab_sc[48 + 32 * u : 64 + 32 * u, :].bitcast(I32), scale_rows[u].bitcast(I32))
+            nc.sync.dma_start(tab_sc[48 + 32 * u : 64 + 32 * u, 0:T].bitcast(I32), scale_rows[u].bitcast(I32))
         tab_w = [placed(f"tab_w{a}", [P, T], U32, TABLE_AT[a]) for a in range(2)]
 
         def load_table(a):
@@ -107,7 +108,7 @@ def tile_list_rumour_cascade_scores_kernel(
         nc.scalar.activation(warm[:, 0:1], log_gain[:, 0:1], ACT.Exp)
 
         picked_sc = keep.tile([P, S], U8, name="picked_sc", align_bytes=64)
-        nc.vector.tensor_copy(picked_sc[:], tab_sc[:].indirect(offs_t[:]))
+        nc.vector.tensor_copy(picked_sc[:], tab_sc[:, 0:T].indirect(offs_t[:]))
         for a in range(2):
             for h in range(2):
                 first = 48 + 4 * (2 * a + h)
@@ -239,21 +240,23 @@ def tile_list_rumour_cascade_scores_kernel(
         turned_early = turned_tile(1, EARLY)
         turned_late = turned_tile(1, LATE)
 
-        pooled = placed("pooled", [P, 8, SHARES], F32, W2_AT[1])
-        for k, x_bank in enumerate((0, 1, 2, 5)):
-            own = piece("own", k, EVERY)
-            nc.vector.tensor_copy(own[:], picked(k, pos1_t, EVERY))
-            other = piece("other", k, EVERY)
-            nc.vector.tensor_copy(other[:], picked(k, pos2_t, EVERY))
-            base = pooled[:, 4 + k, :]
+        pooled = placed("pooled", [P, 2 * POOL_TILES, SHARES], F32, W2_AT[1])
+        for k, x_bank in enumerate((0, 1, 2, 5, 3, 0)[0:POOL_TILES]):
+            cols, turned = (EVERY, turned_first) if k < 4 else (EARLY, turned_early)
+            own = piece("own", k, cols)
+            nc.vector.tensor_copy(own[:], picked(k, pos1_t, cols))
+            other = piece("other", k, cols)
+            nc.vector.tensor_copy(other[:], picked(k, pos2_t, cols))
+            base, diff = pooled[:, 2 * k, cols], pooled[:, 2 * k + 1, cols]
             nc.gpsimd.tensor_scalar(base, own[:], -1.0, log_gain[:, k : k + 1], ALU.mult, ALU.add)
-            nc.gpsimd.tensor_tensor(pooled[:, k, :], own[:], other[:], ALU.subtract)
-            excess = piece("excess", k, EVERY)
-            nc.scalar.activation(excess[:], pooled[:, k, :], ACT.Relu)
-            x = bank(x_bank, [P, 4, P])
+            nc.gpsimd.tensor_tensor(diff, own[:], other[:], ALU.subtract)
+            excess = piece("excess", k, cols)
+            nc.scalar.activation(excess[:], diff, ACT.Relu)
+            x = bank(x_bank, [P, cols.stop // P, P])
             add_turned(x, base, excess)
-            bell(k, x[:], turned_first, 1.0)
-        first_z = [turn_back(0, turned_first, EVERY, 2 * n, 2, 6 + n, nc.scalar.copy) for n in range(2)]
+            bell(k, x[:], turned, 1.0)
+            if k == 3:
+                first_z = [turn_back(0, turned_first, EVERY, 2 * n, 2, 6 + n, nc.scalar.copy) for n in range(2)]
 
         owns, gaps, cuts = {}, {}, {}
 
@@ -276,11 +279,11 @@ def tile_list_rumour_cascade_scores_kernel(
             bell(k, x, turned, -1.0)
 
         early_blocks = EARLY.stop // P
-        for k in range(4, 8):
+        for k in range(POOL_TILES, 8):
             pick_own(k, EARLY, piece("own", k, EARLY)[:])
-        early_gaps = keep.tile([P, 4, EARLY.stop], F32, name="early_gaps", tag="other3_0", align_bytes=64)
-        pick_gap(4, EARLY, early_gaps[:, 0, :])
-        for k in range(5, 8):
+        early_gaps = keep.tile([P, 4, EARLY.stop], F32, name="early_gaps", tag=f"other{POOL_TILES - 1}_0", align_bytes=64)
+        pick_gap(POOL_TILES, EARLY, early_gaps[:, POOL_TILES - 4, :])
+        for k in range(POOL_TILES + 1, 8):
             pick_gap(k, EARLY, early_gaps[:, k - 4, :])
             clip(k - 1, EARLY)
             respond(k - 1, EARLY, bank(k - 5, [P, early_blocks, P])[:], turned_early)
@@ -348,25 +351,45 @@ def tile_list_rumour_cascade_scores_kernel(
             ys[j] = keep.tile([P, SHARES], F32, name="y", tag=tag)
             copy(ys[j][:], accs[j][:])
 
-        def damping(j):
+        def parts(j):
+            return [slice(0, P), slice(P, PAIRS)] if j == 3 else [slice(0, PAIRS)]
+
+        sizes, roots = {}, {}
+
+        def size(j):
             right = keep.tile([P, PAIRS], F32, name="right", tag=f"right{j}")
             nc.vector.tensor_copy(right[:], ys[j][:].indirect(pos4_t[:]))
-            size = keep.tile([P, PAIRS], F32, name=f"size{j}")
-            nc.scalar.activation(size[:], right[:], ACT.Abs)
-            root = keep.tile([P, PAIRS], F32, name=f"root{j}")
-            nc.scalar.activation(root[:], size[:], ACT.Abs_reciprocal_sqrt, bias=1.0)
+            sizes[j] = keep.tile([P, PAIRS], F32, name=f"size{j}")
+            nc.scalar.activation(sizes[j][:], right[:], ACT.Abs)
+
+        def root(j):
+            roots[j] = keep.tile([P, PAIRS], F32, name=f"root{j}")
+            for cols in parts(j):
+                nc.scalar.activation(roots[j][:, cols], sizes[j][:, cols], ACT.Abs_reciprocal_sqrt, bias=1.0)
+
+        def damp(j):
             damps[j] = keep.tile([P, PAIRS], F32, name=f"damp{j}")
-            nc.scalar.activation(damps[j][:], root[:], ACT.Square)
+            for cols in parts(j):
+                nc.scalar.activation(damps[j][:, cols], roots[j][:, cols], ACT.Square)
 
         leave(0, nc.vector.tensor_copy, "y0")
         leave(1, nc.scalar.copy, "y1")
         leave(2, nc.scalar.copy, "y2")
-        for j in range(2):
-            damping(j)
+        size(0)
+        size(1)
         leave(3, nc.vector.tensor_copy, "right0")
-        for j in range(2, 4):
-            damping(j)
+        root(0)
+        root(1)
+        damp(0)
+        size(2)
+        damp(1)
+        root(2)
+        size(3)
+        damp(2)
+        root(3)
+        damp(3)
         for j in range(N // P):
             res = keep.tile([P, PAIRS], F32, name=f"res{j}")
-            nc.vector.tensor_tensor(res[:], ys[j][:].indirect(pos3_t[:]), damps[j][:], ALU.mult)
-            nc.sync.dma_start(out[P * j : P * (j + 1), :], res[:])
+            for cols in parts(j):
+                nc.vector.tensor_tensor(res[:, cols], ys[j][:].indirect(entries(pos3_t, cols)), damps[j][:, cols], ALU.mult)
+                nc.sync.dma_start(out[P * j : P * (j + 1), cols], res[:, cols])

@@ -56,8 +56,9 @@ def tile_list_rumour_cascade_scores_kernel(
         def entries(lst, cols):
             return lst[:, cols.start // 16 : cols.stop // 16]
 
-        w1_sc = keep.tile([P, 2 * H], U8, name="w1_sc", align_bytes=64)
-        nc.gpsimd.memset(w1_sc[:].bitcast(I32), 0)
+        w1_sc = [keep.tile([P, 2 * PASS], U8, name=f"w1_sc{b}", align_bytes=64) for b in range(2)]
+        for b in range(2):
+            nc.gpsimd.memset(w1_sc[b][:].bitcast(I32), 0)
         tab_sc = placed("tab_sc", [P, T + 4], U8, 0)
         for first, last in ((0, 48), (64, 80), (96, P)):
             nc.vector.memset(tab_sc[first:last, :].bitcast(I32), 0)
@@ -75,27 +76,32 @@ def tile_list_rumour_cascade_scores_kernel(
         def load_table(a):
             nc.sync.dma_start(tab_w[a][:].bitcast(I32), tab_words[a].rearrange("p t i -> p (t i)").bitcast(I32))
 
-        def load_w1_scales(q):
+        def load_w1_scales(b, q):
             nc.sync.dma_start(
-                w1_sc[32 * q : 32 * q + 4, :].bitcast(I32),
-                w1_scales[:, 4 * q : 4 * q + 4, :].rearrange("a r c -> r a c").bitcast(I32),
+                w1_sc[b][32 * q : 32 * q + 4, :].bitcast(I32),
+                w1_scales[:, 4 * q : 4 * q + 4, PASS * b : PASS * (b + 1)].rearrange("a r c -> r a c").bitcast(I32),
             )
 
-        load_w1_scales(0)
-        load_w1_scales(1)
+        load_w1_scales(0, 0)
+        load_w1_scales(0, 2)
         load_table(0)
 
-        def load_w1(b, words):
+        w1_w = {}
+
+        def load_w1(first, last, make):
+            width = 2 * P * (last - first)
+            words = make([P, 2, width])
             nc.sync.dma_start(
-                words[:].bitcast(I32).rearrange("p (a c) -> p a c", a=2),
-                w1_words[:, :, H * b : H * (b + 1)].rearrange("a p c -> p a c").bitcast(I32),
+                words[:].rearrange("p a c -> p (a c)").bitcast(I32),
+                w1_words[:, :, 2 * P * first : 2 * P * last].rearrange("a p c -> p a c").bitcast(I32),
             )
-            return words
+            for k in range(first, last):
+                w1_w[k] = words[:, :, 2 * P * (k - first) : 2 * P * (k - first + 1)]
 
         load_table(1)
-        w1_w = [load_w1(0, keep.tile([P, 2 * H], U8, name="w1_first", align_bytes=64))]
-        load_w1_scales(2)
-        load_w1_scales(3)
+        load_w1(0, 1, lambda shape: keep.tile(shape, U8, name="w1_first", align_bytes=64))
+        load_w1_scales(0, 1)
+        load_w1_scales(0, 3)
         warm = keep.tile([P, 24], F32, name="warm")
         nc.scalar.activation(warm[0:96, 16:17], gain_rows[0:96, 0:1], ACT.Ln, bias=1.0)
         ident = keep.tile([P, P], F32, name="ident")
@@ -130,20 +136,23 @@ def tile_list_rumour_cascade_scores_kernel(
         halves = [slice(0, BANK_COLS), slice(BANK_COLS, S)]
         first_pieces = [halves[0], slice(BANK_COLS, BANK_COLS + 256), slice(BANK_COLS + 256, S)]
         pick_words(0, slice(0, S))
+        load_w1(1, 4, lambda shape: keep.tile(shape, U8, name="w1_next", align_bytes=64))
         pos1_t = load_list(pos1, "pos1_t")
         pos2_t = load_list(pos2, "pos2_t")
-        w2_raw = [load_w2(0), load_w2(1)]
+        w2_raw = [load_w2(0)]
+        for q in (0, 2, 1, 3):
+            load_w1_scales(1, q)
+        w2_raw.append(load_w2(1))
         pos3_t = load_list(pos3, "pos3_t")
         pos4_t = load_list(pos4, "pos4_t")
         for cols in first_pieces:
             pick_words(1, cols)
-        w1_w.append(load_w1(1, placed("w1_second", [P, 2 * H], U8, TABLE_AT[1])))
+        load_w1(4, 8, lambda shape: placed("w1_last", shape, U8, TABLE_AT[1]))
         w2_raw.extend([load_w2(2), load_w2(3)])
 
         sqs = [keep.tile([P, S], F32, name=f"sq{k}") for k in range(ROW_TILES)]
 
         def square(k, cols, d_bank):
-            b, t = divmod(k, 4)
             width = cols.stop - cols.start
             step = width if width == BANK_COLS else P
             d = bank(d_bank, [P, width])
@@ -153,8 +162,8 @@ def tile_list_rumour_cascade_scores_kernel(
                     part = slice(cols.start + c, cols.start + c + step)
                     nc.tensor.matmul_mx(
                         out=d[:, c : c + step],
-                        lhsT=w1_w[b][:, H * a + 2 * P * t : H * a + 2 * P * (t + 1)].bitcast(FP4X4),
-                        lhsT_scale=w1_sc[:, H * a + P * k : H * a + P * (k + 1)],
+                        lhsT=w1_w[k][:, a, :].bitcast(FP4X4),
+                        lhsT_scale=w1_sc[k // 4][:, PASS * a + P * (k % 4) : PASS * a + P * (k % 4 + 1)],
                         rhs=v_w[a][:, part].bitcast(FP8X4),
                         rhs_scale=v_sc[a][:, part],
                         start=(a == order[0] and c == 0),

@@ -24,10 +24,15 @@ BANK_BYTES = 2048
 ROW_TILES = H // P
 D_BANKS = 6
 
-TABLE_AT = (12352, 2112)
-W2_AT = (12352, 16448, 4160, 8256)
-LAST_GAP_AT = 43008
 POOL_TILES = 5
+
+QUARTER = 4 * 4 * (N // 2)
+LAST_PASS_AT = T
+FIRST_PASS_AT = LAST_PASS_AT + 2 * H + 2 * QUARTER
+TABLE_AT = (FIRST_PASS_AT, LAST_PASS_AT)
+W2_AT = (FIRST_PASS_AT, FIRST_PASS_AT + QUARTER, LAST_PASS_AT + 2 * H, LAST_PASS_AT + 2 * H + QUARTER)
+POOLED_AT = W2_AT[1]
+LAST_GAP_AT = 42 * 1024
 
 EVERY = slice(0, SHARES)
 EARLY, LATE = slice(0, SHARES - P), slice(SHARES - P, SHARES)
@@ -59,7 +64,7 @@ def tile_list_rumour_cascade_scores_kernel(
         w1_sc = [keep.tile([P, 2 * PASS], U8, name=f"w1_sc{b}", align_bytes=64) for b in range(2)]
         for b in range(2):
             nc.gpsimd.memset(w1_sc[b][:].bitcast(I32), 0)
-        tab_sc = placed("tab_sc", [P, T + 4], U8, 0)
+        tab_sc = placed("tab_sc", [P, T], U8, 0)
         for first, last in ((0, 48), (64, 80), (96, P)):
             nc.vector.memset(tab_sc[first:last, :].bitcast(I32), 0)
         gain_rows = keep.tile([P, P], F32, name="gain_rows")
@@ -70,7 +75,7 @@ def tile_list_rumour_cascade_scores_kernel(
         offs_t = load_list(offs, "offs_t")
         scale_rows = tab_scales.rearrange("a (h u j) t -> u (a h) j t", h=2, u=2)
         for u in range(2):
-            nc.sync.dma_start(tab_sc[48 + 32 * u : 64 + 32 * u, 0:T].bitcast(I32), scale_rows[u].bitcast(I32))
+            nc.sync.dma_start(tab_sc[48 + 32 * u : 64 + 32 * u, :].bitcast(I32), scale_rows[u].bitcast(I32))
         tab_w = [placed(f"tab_w{a}", [P, T], U32, TABLE_AT[a]) for a in range(2)]
 
         def load_table(a):
@@ -88,9 +93,7 @@ def tile_list_rumour_cascade_scores_kernel(
 
         w1_w = {}
 
-        def load_w1(first, last, make):
-            width = 2 * P * (last - first)
-            words = make([P, 2, width])
+        def load_w1(first, last, words):
             nc.sync.dma_start(
                 words[:].rearrange("p a c -> p (a c)").bitcast(I32),
                 w1_words[:, :, 2 * P * first : 2 * P * last].rearrange("a p c -> p a c").bitcast(I32),
@@ -99,7 +102,7 @@ def tile_list_rumour_cascade_scores_kernel(
                 w1_w[k] = words[:, :, 2 * P * (k - first) : 2 * P * (k - first + 1)]
 
         load_table(1)
-        load_w1(0, 1, lambda shape: keep.tile(shape, U8, name="w1_first", align_bytes=64))
+        load_w1(0, 1, keep.tile([P, 2, 2 * P], U8, name="w1_first", align_bytes=64))
         load_w1_scales(0, 1)
         load_w1_scales(0, 3)
         warm = keep.tile([P, 24], F32, name="warm")
@@ -114,7 +117,7 @@ def tile_list_rumour_cascade_scores_kernel(
         nc.scalar.activation(warm[:, 0:1], log_gain[:, 0:1], ACT.Exp)
 
         picked_sc = keep.tile([P, S], U8, name="picked_sc", align_bytes=64)
-        nc.vector.tensor_copy(picked_sc[:], tab_sc[:, 0:T].indirect(offs_t[:]))
+        nc.vector.tensor_copy(picked_sc[:], tab_sc[:].indirect(offs_t[:]))
         for a in range(2):
             for h in range(2):
                 first = 48 + 4 * (2 * a + h)
@@ -134,9 +137,9 @@ def tile_list_rumour_cascade_scores_kernel(
             nc.vector.tensor_copy(v_w[a][:, cols], tab_w[a][:].indirect(entries(offs_t, cols)))
 
         halves = [slice(0, BANK_COLS), slice(BANK_COLS, S)]
-        first_pieces = [halves[0], slice(BANK_COLS, BANK_COLS + 256), slice(BANK_COLS + 256, S)]
+        first_pieces = [halves[0], slice(BANK_COLS, S - T // 8), slice(S - T // 8, S)]
         pick_words(0, slice(0, S))
-        load_w1(1, 4, lambda shape: keep.tile(shape, U8, name="w1_next", align_bytes=64))
+        load_w1(1, 4, keep.tile([P, 2, 3 * 2 * P], U8, name="w1_next", align_bytes=64))
         pos1_t = load_list(pos1, "pos1_t")
         pos2_t = load_list(pos2, "pos2_t")
         w2_raw = [load_w2(0)]
@@ -147,7 +150,7 @@ def tile_list_rumour_cascade_scores_kernel(
         pos4_t = load_list(pos4, "pos4_t")
         for cols in first_pieces:
             pick_words(1, cols)
-        load_w1(4, 8, lambda shape: placed("w1_last", shape, U8, TABLE_AT[1]))
+        load_w1(4, ROW_TILES, placed("w1_last", [P, 2, 4 * 2 * P], U8, LAST_PASS_AT))
         w2_raw.extend([load_w2(2), load_w2(3)])
 
         sqs = [keep.tile([P, S], F32, name=f"sq{k}") for k in range(ROW_TILES)]
@@ -200,7 +203,7 @@ def tile_list_rumour_cascade_scores_kernel(
             )
 
         z_w = [keep.tile([P, SHARES], U32, name=f"z_w{b}", align_bytes=64) for b in range(2)]
-        z_planes = placed("z_planes", [P, 2 * SHARES], U8, LAST_GAP_AT - 768)
+        z_planes = placed("z_planes", [P, 2 * SHARES], U8, LAST_GAP_AT + 2 * P - 2 * SHARES)
         z_sc = [z_planes[:, SHARES * b : SHARES * (b + 1)] for b in range(2)]
 
         def piece(name, k, cols):
@@ -249,8 +252,8 @@ def tile_list_rumour_cascade_scores_kernel(
         turned_early = turned_tile(1, EARLY)
         turned_late = turned_tile(1, LATE)
 
-        pooled = placed("pooled", [P, 2 * POOL_TILES, SHARES], F32, W2_AT[1])
-        for k, x_bank in enumerate((0, 1, 2, 5, 3, 0)[0:POOL_TILES]):
+        pooled = placed("pooled", [P, 2 * POOL_TILES, SHARES], F32, POOLED_AT)
+        for k, x_bank in enumerate((0, 1, 2, 5, 3)):
             cols, turned = (EVERY, turned_first) if k < 4 else (EARLY, turned_early)
             own = piece("own", k, cols)
             nc.vector.tensor_copy(own[:], picked(k, pos1_t, cols))
@@ -288,25 +291,27 @@ def tile_list_rumour_cascade_scores_kernel(
             bell(k, x, turned, -1.0)
 
         early_blocks = EARLY.stop // P
-        for k in range(POOL_TILES, 8):
+        for k in range(POOL_TILES, ROW_TILES):
             pick_own(k, EARLY, piece("own", k, EARLY)[:])
-        early_gaps = keep.tile([P, 4, EARLY.stop], F32, name="early_gaps", tag=f"other{POOL_TILES - 1}_0", align_bytes=64)
+        early_gaps = keep.tile(
+            [P, 4, EARLY.stop], F32, name="early_gaps", tag=f"other{POOL_TILES - 1}_0", align_bytes=64
+        )
         pick_gap(POOL_TILES, EARLY, early_gaps[:, POOL_TILES - 4, :])
-        for k in range(POOL_TILES + 1, 8):
+        for k in range(POOL_TILES + 1, ROW_TILES):
             pick_gap(k, EARLY, early_gaps[:, k - 4, :])
             clip(k - 1, EARLY)
             respond(k - 1, EARLY, bank(k - 5, [P, early_blocks, P])[:], turned_early)
         for c in range(0, N, P):
             nc.scalar.copy(
                 w2_grouped[1][:, c : c + P, :].rearrange("p (c i) t -> p c t i", i=4),
-                w2_raw[2 + c // 256][:, :, c % 256 : c % 256 + P].rearrange("p t (c i) -> p c t i", i=4),
+                w2_raw[2 + c // (N // 2)][:, :, c % (N // 2) : c % (N // 2) + P].rearrange("p t (c i) -> p c t i", i=4),
             )
-        late_owns = placed("late_owns", [P, 4, P], F32, W2_AT[1])
+        late_owns = placed("late_owns", [P, 4, P], F32, POOLED_AT)
         pick_own(4, LATE, late_owns[:, 0, :])
         clip(7, EARLY)
         pair = psum.tile([P, 2, 4, P], F32, name="pair", offset=BANK_BYTES * 4)
         respond(7, EARLY, pair[:, 0, 0:early_blocks, :], turned_early)
-        for k in range(5, 8):
+        for k in range(5, ROW_TILES):
             pick_own(k, LATE, late_owns[:, k - 4, :])
         early_z = [
             turn_back(1, turned_early, EARLY, 0, 2, 6, nc.scalar.copy),
@@ -314,8 +319,9 @@ def tile_list_rumour_cascade_scores_kernel(
         ]
 
         pick_gap(4, LATE, piece("gap", 4, LATE)[:])
-        for k in range(5, 8):
-            pick_gap(k, LATE, (placed("last_gap", [P, P], F32, LAST_GAP_AT) if k == 7 else piece("gap", k, LATE))[:])
+        for k in range(5, ROW_TILES):
+            gap = placed("last_gap", [P, P], F32, LAST_GAP_AT) if k == ROW_TILES - 1 else piece("gap", k, LATE)
+            pick_gap(k, LATE, gap[:])
             clip(k - 1, LATE)
         three = bank(5, [P, 3, P])
         for n, terms in enumerate((owns, cuts)):
@@ -332,18 +338,16 @@ def tile_list_rumour_cascade_scores_kernel(
         respond(7, LATE, wide[:, 3, 0:1, :], turned_late)
         for made in first_z:
             quantize_z(*made)
-        quantize_w2(0, placed("w2_planes", [P, N], U8, LAST_GAP_AT + 256))
+        quantize_w2(0, placed("w2_planes", [P, N], U8, LAST_GAP_AT + 2 * P))
         quantize_z(*early_z[0])
         late_z = turn_back(1, turned_late, LATE, 0, 1, 0, nc.scalar.copy)
         quantize_z(*early_z[1])
         quantize_z(*late_z)
         warm_root = keep.tile([P, 8], F32, name="warm_root", tag=f"turned1_{LATE.start}")
         nc.scalar.activation(warm_root[:, 0:1], log_gain[:, 0:1], ACT.Abs_reciprocal_sqrt, bias=1.0)
-
         quantize_w2(1, keep.tile([P, N], U8, name="w2_right", tag=f"z1_{LATE.start}", align_bytes=64))
 
         accs = [bank(j + 1, [P, SHARES]) for j in range(N // P)]
-        ys, damps = {}, {}
         for j in range(N // P):
             for b in range(2):
                 nc.tensor.matmul_mx(
@@ -356,14 +360,14 @@ def tile_list_rumour_cascade_scores_kernel(
                     stop=(b == 1),
                 )
 
+        ys, sizes, roots, damps = {}, {}, {}, {}
+
         def leave(j, copy, tag):
             ys[j] = keep.tile([P, SHARES], F32, name="y", tag=tag)
             copy(ys[j][:], accs[j][:])
 
         def parts(j):
-            return [slice(0, P), slice(P, PAIRS)] if j == 3 else [slice(0, PAIRS)]
-
-        sizes, roots = {}, {}
+            return [slice(0, P), slice(P, PAIRS)] if j == N // P - 1 else [slice(0, PAIRS)]
 
         def size(j):
             right = keep.tile([P, PAIRS], F32, name="right", tag=f"right{j}")
@@ -400,5 +404,6 @@ def tile_list_rumour_cascade_scores_kernel(
         for j in range(N // P):
             res = keep.tile([P, PAIRS], F32, name=f"res{j}")
             for cols in parts(j):
-                nc.vector.tensor_tensor(res[:, cols], ys[j][:].indirect(entries(pos3_t, cols)), damps[j][:, cols], ALU.mult)
+                left = ys[j][:].indirect(entries(pos3_t, cols))
+                nc.vector.tensor_tensor(res[:, cols], left, damps[j][:, cols], ALU.mult)
                 nc.sync.dma_start(out[P * j : P * (j + 1), cols], res[:, cols])

@@ -24,6 +24,7 @@ BANK_BYTES = 2048
 ROW_TILES = H // P
 D_BANKS = 6
 
+SCALE_ROWS_AT = P - 32
 POOL_TILES = 5
 
 QUARTER = 4 * 4 * (N // 2)
@@ -65,17 +66,16 @@ def tile_list_rumour_cascade_scores_kernel(
         for b in range(2):
             nc.gpsimd.memset(w1_sc[b][:].bitcast(I32), 0)
         tab_sc = placed("tab_sc", [P, T], U8, 0)
-        for first, last in ((0, 48), (64, 80), (96, P)):
-            nc.vector.memset(tab_sc[first:last, :].bitcast(I32), 0)
+        nc.vector.memset(tab_sc[0:SCALE_ROWS_AT, :].bitcast(I32), 0)
         gain_rows = keep.tile([P, P], F32, name="gain_rows")
         nc.scalar.dma_start(gain_rows[P - ROW_TILES : P, :], gain.rearrange("(k p) -> k p", p=P))
         nc.gpsimd.memset(gain_rows[0:96, :], 0.0)
         nc.gpsimd.memset(gain_rows[96 : P - ROW_TILES, :], 0.0)
 
+        nc.sync.dma_start(
+            tab_sc[SCALE_ROWS_AT:P, :].bitcast(I32), tab_scales.rearrange("a q t -> (a q) t").bitcast(I32)
+        )
         offs_t = load_list(offs, "offs_t")
-        scale_rows = tab_scales.rearrange("a (h u j) t -> u (a h) j t", h=2, u=2)
-        for u in range(2):
-            nc.sync.dma_start(tab_sc[48 + 32 * u : 64 + 32 * u, :].bitcast(I32), scale_rows[u].bitcast(I32))
         tab_w = [placed(f"tab_w{a}", [P, T], U32, TABLE_AT[a]) for a in range(2)]
 
         def load_table(a):
@@ -101,10 +101,10 @@ def tile_list_rumour_cascade_scores_kernel(
             for k in range(first, last):
                 w1_w[k] = words[:, :, 2 * P * (k - first) : 2 * P * (k - first + 1)]
 
-        load_table(1)
-        load_w1(0, 1, keep.tile([P, 2, 2 * P], U8, name="w1_first", align_bytes=64))
         load_w1_scales(0, 1)
         load_w1_scales(0, 3)
+        load_w1(0, 1, keep.tile([P, 2, 2 * P], U8, name="w1_first", align_bytes=64))
+        load_table(1)
         warm = keep.tile([P, 24], F32, name="warm")
         nc.scalar.activation(warm[0:96, 16:17], gain_rows[0:96, 0:1], ACT.Ln, bias=1.0)
         ident = keep.tile([P, P], F32, name="ident")
@@ -113,16 +113,18 @@ def tile_list_rumour_cascade_scores_kernel(
         nc.tensor.transpose(gain_cols[:], gain_rows[:], ident[:])
         log_gain = keep.tile([P, ROW_TILES], F32, name="log_gain")
         nc.scalar.activation(log_gain[:], gain_cols[:, P - ROW_TILES : P], ACT.Ln)
-        v_sc = [keep.tile([P, S], U8, name=f"v_sc{a}", align_bytes=64) for a in range(2)]
+        planes = keep.tile([P, 2 * S], U8, name="planes", align_bytes=64)
+        nc.gpsimd.memset(planes[:].bitcast(I32), 0)
+        v_sc = [planes[:, S * a : S * (a + 1)] for a in range(2)]
         nc.scalar.activation(warm[:, 0:1], log_gain[:, 0:1], ACT.Exp)
 
         picked_sc = keep.tile([P, S], U8, name="picked_sc", align_bytes=64)
         nc.vector.tensor_copy(picked_sc[:], tab_sc[:].indirect(offs_t[:]))
         for a in range(2):
-            for h in range(2):
-                first = 48 + 4 * (2 * a + h)
+            for q in range(4):
+                first = SCALE_ROWS_AT + 16 * a + 4 * q
                 nc.sync.dma_start(
-                    v_sc[a][64 * h : 64 * (h + 1), :].bitcast(I32), picked_sc[first : first + 64, :].bitcast(I32)
+                    v_sc[a][32 * q : 32 * q + 4, :].bitcast(I32), picked_sc[first : first + 4, :].bitcast(I32)
                 )
 
         def load_w2(n):

@@ -87,9 +87,10 @@ def tile_list_rumour_cascade_scores_kernel(
                 w1_scales[:, 4 * q : 4 * q + 4, PASS * b : PASS * (b + 1)].rearrange("a r c -> r a c").bitcast(I32),
             )
 
-        load_w1_scales(0, 0)
-        load_w1_scales(0, 2)
         load_table(0)
+        for q in (0, 2, 1, 3):
+            load_w1_scales(0, q)
+        load_table(1)
 
         w1_w = {}
 
@@ -101,10 +102,7 @@ def tile_list_rumour_cascade_scores_kernel(
             for k in range(first, last):
                 w1_w[k] = words[:, :, 2 * P * (k - first) : 2 * P * (k - first + 1)]
 
-        load_w1_scales(0, 1)
-        load_w1_scales(0, 3)
         load_w1(0, 1, keep.tile([P, 2, 2 * P], U8, name="w1_first", align_bytes=64))
-        load_table(1)
         warm = keep.tile([P, 24], F32, name="warm")
         nc.scalar.activation(warm[0:96, 16:17], gain_rows[0:96, 0:1], ACT.Ln, bias=1.0)
         ident = keep.tile([P, P], F32, name="ident")

from contextlib import ExitStack

import concourse.mybir as mybir
from concourse.masks import make_identity

K, H, N, T, S, SHARES, PAIRS = 1024, 1024, 512, 2048, 1024, 512, 256
FLOPS = 2 * K * H * S + 2 * H * N * SHARES

F32 = mybir.dt.float32
BF16 = mybir.dt.bfloat16
I32 = mybir.dt.int32
U32 = mybir.dt.uint32
U16 = mybir.dt.uint16
U8 = mybir.dt.uint8
FP8X4 = mybir.dt.float8_e4m3fn_x4
FP4X4 = mybir.dt.float4_e2m1fn_x4
ACT = mybir.ActivationFunctionType
ALU = mybir.AluOpType

P = 128
PASS = 512
BANK_COLS = 512
BANK_BYTES = 2048
ROW_TILES = H // P
D_BANKS = 6

SCALE_ROWS_AT = P - 32
POOL_TILES = 5

QUARTER = 4 * 4 * (N // 2)
LAST_PASS_AT = T
FIRST_PASS_AT = LAST_PASS_AT + 2 * H + 2 * QUARTER
TABLE_AT = (FIRST_PASS_AT, LAST_PASS_AT)
W2_AT = (FIRST_PASS_AT, FIRST_PASS_AT + QUARTER, LAST_PASS_AT + 2 * H, LAST_PASS_AT + 2 * H + QUARTER)
POOLED_AT = W2_AT[1]
LAST_GAP_AT = 42 * 1024

EVERY = slice(0, SHARES)
EARLY, LATE = slice(0, SHARES - P), slice(SHARES - P, SHARES)


def tile_list_rumour_cascade_scores_kernel(
    tc, tab_words, tab_scales, offs, w1_words, w1_scales, gain, pos1, pos2, w2, pos3, pos4, out
):
    nc = tc.nc
    with ExitStack() as ctx:
        keep = ctx.enter_context(tc.tile_pool(name="keep", bufs=1))
        stage = ctx.enter_context(tc.tile_pool(name="stage", bufs=1))
        psum = ctx.enter_context(tc.psum_pool(name="psum", bufs=1))

        def bank(index, shape):
            return psum.tile(shape, F32, name="bank", tag=f"bank{index}", offset=BANK_BYTES * index)

        def placed(name, shape, dtype, at):
            return stage.tile(shape, dtype, name=name, offset=at, align_bytes=64)

        def load_list(src, name):
            lst = keep.tile([P, src.shape[1]], U16, name=name)
            nc.sync.dma_start(lst[:], src)
            return lst

        def entries(lst, cols):
            return lst[:, cols.start // 16 : cols.stop // 16]

        w1_sc = [keep.tile([P, 2 * PASS], U8, name=f"w1_sc{b}", align_bytes=64) for b in range(2)]
        for b in range(2):
            nc.gpsimd.memset(w1_sc[b][:].bitcast(I32), 0)
        tab_sc = placed("tab_sc", [P, T], U8, 0)
        nc.vector.memset(tab_sc[0:SCALE_ROWS_AT, :].bitcast(I32), 0)
        gain_rows = keep.tile([P, P], F32, name="gain_rows")
        nc.scalar.dma_start(gain_rows[P - ROW_TILES : P, :], gain.rearrange("(k p) -> k p", p=P))
        nc.gpsimd.memset(gain_rows[0:96, :], 0.0)
        nc.gpsimd.memset(gain_rows[96 : P - ROW_TILES, :], 0.0)

        nc.sync.dma_start(
            tab_sc[SCALE_ROWS_AT:P, :].bitcast(I32), tab_scales.rearrange("a q t -> (a q) t").bitcast(I32)
        )
        offs_t = load_list(offs, "offs_t")
        tab_w = [placed(f"tab_w{a}", [P, T], U32, TABLE_AT[a]) for a in range(2)]

        def load_table(a):
            nc.sync.dma_start(tab_w[a][:].bitcast(I32), tab_words[a].rearrange("p t i -> p (t i)").bitcast(I32))

        def load_w1_scales(b, q):
            nc.sync.dma_start(
                w1_sc[b][32 * q : 32 * q + 4, :].bitcast(I32),
                w1_scales[:, 4 * q : 4 * q + 4, PASS * b : PASS * (b + 1)].rearrange("a r c -> r a c").bitcast(I32),
            )

        load_table(0)
        for q in (0, 2, 1, 3):
            load_w1_scales(0, q)
        load_table(1)

        w1_w = {}

        def load_w1(first, last, words):
            nc.sync.dma_start(
                words[:].rearrange("p a c -> p (a c)").bitcast(I32),
                w1_words[:, :, 2 * P * first : 2 * P * last].rearrange("a p c -> p a c").bitcast(I32),
            )
            for k in range(first, last):
                w1_w[k] = words[:, :, 2 * P * (k - first) : 2 * P * (k - first + 1)]

        load_w1(0, 1, keep.tile([P, 2, 2 * P], U8, name="w1_first", align_bytes=64))
        warm = keep.tile([P, 24], F32, name="warm")
        nc.scalar.activation(warm[0:96, 16:17], gain_rows[0:96, 0:1], ACT.Ln, bias=1.0)
        ident = keep.tile([P, P], F32, name="ident")
        make_identity(nc, ident[:])
        gain_cols = bank(6, [P, P])
        nc.tensor.transpose(gain_cols[:], gain_rows[:], ident[:])
        log_gain = keep.tile([P, ROW_TILES], F32, name="log_gain")
        nc.scalar.activation(log_gain[:], gain_cols[:, P - ROW_TILES : P], ACT.Ln)
        planes = keep.tile([P, 2 * S], U8, name="planes", align_bytes=64)
        nc.gpsimd.memset(planes[:].bitcast(I32), 0)
        v_sc = [planes[:, S * a : S * (a + 1)] for a in range(2)]
        nc.scalar.activation(warm[:, 0:1], log_gain[:, 0:1], ACT.Exp)

        picked_sc = keep.tile([P, S], U8, name="picked_sc", align_bytes=64)
        nc.vector.tensor_copy(picked_sc[:], tab_sc[:].indirect(offs_t[:]))
        for a in range(2):
            for q in range(4):
                first = SCALE_ROWS_AT + 16 * a + 4 * q
                nc.sync.dma_start(
                    v_sc[a][32 * q : 32 * q + 4, :].bitcast(I32), picked_sc[first : first + 4, :].bitcast(I32)
                )

        def load_w2(n):
            b, cols = n // 2, slice(N // 2 * (n % 2), N // 2 * (n % 2 + 1))
            raw = placed(f"w2_raw{n}", [P, 4, N // 2], F32, W2_AT[n])
            nc.sync.dma_start(raw[:], w2[PASS * b : PASS * (b + 1), cols].rearrange("(p j) n -> p j n", j=4))
            return raw

        v_w = [keep.tile([P, S], U32, name=f"v_w{a}", align_bytes=64) for a in range(2)]

        def pick_words(a, cols):
            nc.vector.tensor_copy(v_w[a][:, cols], tab_w[a][:].indirect(entries(offs_t, cols)))

        halves = [slice(0, BANK_COLS), slice(BANK_COLS, S)]
        first_pieces = [halves[0], slice(BANK_COLS, S - T // 8), slice(S - T // 8, S)]
        pick_words(0, slice(0, S))
        load_w1(1, 4, keep.tile([P, 2, 3 * 2 * P], U8, name="w1_next", align_bytes=64))
        pos1_t = load_list(pos1, "pos1_t")
        pos2_t = load_list(pos2, "pos2_t")
        w2_raw = [load_w2(0)]
        for q in (0, 2, 1, 3):
            load_w1_scales(1, q)
        w2_raw.append(load_w2(1))
        pos3_t = load_list(pos3, "pos3_t")
        pos4_t = load_list(pos4, "pos4_t")
        for cols in first_pieces:
            pick_words(1, cols)
        load_w1(4, ROW_TILES, placed("w1_last", [P, 2, 4 * 2 * P], U8, LAST_PASS_AT))
        w2_raw.extend([load_w2(2), load_w2(3)])

        sqs = [keep.tile([P, S], F32, name=f"sq{k}") for k in range(ROW_TILES)]

        def square(k, cols, d_bank):
            width = cols.stop - cols.start
            step = width if width == BANK_COLS else P
            d = bank(d_bank, [P, width])
            order = (0, 1) if k == 0 else (1, 0)
            for a in order:
                for c in range(0, width, step):
                    part = slice(cols.start + c, cols.start + c + step)
                    nc.tensor.matmul_mx(
                        out=d[:, c : c + step],
                        lhsT=w1_w[k][:, a, :].bitcast(FP4X4),
                        lhsT_scale=w1_sc[k // 4][:, PASS * a + P * (k % 4) : PASS * a + P * (k % 4 + 1)],
                        rhs=v_w[a][:, part].bitcast(FP8X4),
                        rhs_scale=v_sc[a][:, part],
                        start=(a == order[0] and c == 0),
                        stop=(a == order[1] and c + step == width),
                    )
            nc.scalar.activation(sqs[k][:, cols], d[:], ACT.Square)

        d_pieces = [(k, cols) for k in range(ROW_TILES) for cols in (first_pieces if k == 0 else halves)]
        for n, (k, cols) in enumerate(d_pieces):
            square(k, cols, (n + 1) % D_BANKS)

        w2_grouped = [keep.tile([P, N, 4], BF16, name=f"w2_g{b}", align_bytes=64) for b in range(2)]
        w2_w = [keep.tile([P, N], U32, name=f"w2_w{b}", align_bytes=64) for b in range(2)]
        w2_planes = {}

        def quantize_w2(half, planes):
            w2_planes[half] = planes
            cols = slice(N // 2 * half, N // 2 * (half + 1))
            for b in range(2):
                nc.vector.quantize_mx(
                    out=w2_w[b][:, cols].bitcast(FP8X4),
                    scales=planes[:, N // 2 * b : N // 2 * (b + 1)],
                    in_=w2_grouped[b][:, cols, :].rearrange("p n t -> p (n t)"),
                )

        for n in range(2):
            nc.gpsimd.tensor_scalar(
                w2_grouped[0][:, N // 2 * n : N // 2 * (n + 1), :],
                w2_raw[n][:].rearrange("p j n -> p n j"),
                1.0,
                0.0,
                ALU.mult,
                ALU.add,
            )

        z_w = [keep.tile([P, SHARES], U32, name=f"z_w{b}", align_bytes=64) for b in range(2)]
        z_planes = placed("z_planes", [P, 2 * SHARES], U8, LAST_GAP_AT + 2 * P - 2 * SHARES)
        z_sc = [z_planes[:, SHARES * b : SHARES * (b + 1)] for b in range(2)]

        def piece(name, k, cols):
            return keep.tile([P, cols.stop - cols.start], F32, name=f"{name}{k}_{cols.start}", align_bytes=64)

        def picked(k, lst, cols):
            return sqs[k][:].indirect(entries(lst, cols))

        def turn(x, term, start, stop):
            nc.tensor.matmul(x, lhsT=term, rhs=ident[:], is_transpose=True, start=start, stop=stop)

        def add_turned(x, first_term, second_term):
            blocks = x.shape[1]
            for n, term in enumerate((first_term, second_term)):
                for g in range(blocks):
                    turn(x[:, g, :], term[:, P * g : P * (g + 1)], n == 0 and g == 0, n == 1 and g == blocks - 1)

        def turned_tile(b, cols):
            return keep.tile([P, 2, (cols.stop - cols.start) // P, 2 * P], BF16, name=f"turned{b}_{cols.start}")

        def bell(k, x, turned, sign):
            t = k % 4
            nc.scalar.activation(
                turned[:, :, :, 64 * t : 64 * (t + 1)].rearrange("m u g (q e) -> m u g q e", e=2),
                x.rearrange("m g (q u e) -> m u g q e", u=2, e=2),
                ACT.Exp,
                scale=sign,
            )

        def quantize_z(b, z, start):
            part = slice(start, start + z.shape[1] // 4)
            nc.vector.quantize_mx(out=z_w[b][:, part].bitcast(FP8X4), scales=z_sc[b][:, part], in_=z[:])

        def turn_back(b, turned, cols, first_block, blocks, z_bank, copy):
            words = turned[:].rearrange("m u g r -> m (u g r)").bitcast(F32).rearrange("m (u g w) -> m u g w", u=2, w=P)
            back = bank(z_bank, [P, blocks, 2, P])
            for g in range(blocks):
                for u in range(2):
                    nc.tensor.transpose(back[:, g, u, :], words[:, u, first_block + g, :], ident[:])
            start = cols.start + P * first_block
            z = keep.tile([P, blocks * P * 4], BF16, name=f"z{b}_{start}", align_bytes=64)
            copy(z[:].bitcast(F32).rearrange("p (g m u) -> p g m u", u=2, m=P), back[:].rearrange("p g u m -> p g m u"))
            return b, z, start

        turned_first = turned_tile(0, EVERY)
        turned_early = turned_tile(1, EARLY)
        turned_late = turned_tile(1, LATE)

        pooled = placed("pooled", [P, 2 * POOL_TILES, SHARES], F32, POOLED_AT)
        for k, x_bank in enumerate((0, 1, 2, 5, 3)):
            cols, turned = (EVERY, turned_first) if k < 4 else (EARLY, turned_early)
            own = piece("own", k, cols)
            nc.vector.tensor_copy(own[:], picked(k, pos1_t, cols))
            other = piece("other", k, cols)
            nc.vector.tensor_copy(other[:], picked(k, pos2_t, cols))
            base, diff = pooled[:, 2 * k, cols], pooled[:, 2 * k + 1, cols]
            nc.gpsimd.tensor_scalar(base, own[:], -1.0, log_gain[:, k : k + 1], ALU.mult, ALU.add)
            nc.gpsimd.tensor_tensor(diff, own[:], other[:], ALU.subtract)
            excess = piece("excess", k, cols)
            nc.scalar.activation(excess[:], diff, ACT.Relu)
            x = bank(x_bank, [P, cols.stop // P, P])
            add_turned(x, base, excess)
            bell(k, x[:], turned, 1.0)
            if k == 3:
                first_z = [turn_back(0, turned_first, EVERY, 2 * n, 2, 6 + n, nc.scalar.copy) for n in range(2)]

        owns, gaps, cuts = {}, {}, {}

        def pick_own(k, cols, dst):
            owns[k, cols.start] = dst
            nc.vector.tensor_copy(dst, picked(k, pos1_t, cols))

        def pick_gap(k, cols, dst):
            gaps[k, cols.start] = dst
            nc.vector.tensor_tensor(dst, picked(k, pos2_t, cols), owns[k, cols.start], ALU.subtract)

        def clip(k, cols):
            cuts[k, cols.start] = piece("cut", k, cols)[:]
            nc.vector.tensor_scalar(
                cuts[k, cols.start], gaps[k, cols.start], 0.0, log_gain[:, k : k + 1], ALU.min, ALU.subtract
            )

        def respond(k, cols, x, turned):
            add_turned(x, owns[k, cols.start], cuts[k, cols.start])
            bell(k, x, turned, -1.0)

        early_blocks = EARLY.stop // P
        for k in range(POOL_TILES, ROW_TILES):
            pick_own(k, EARLY, piece("own", k, EARLY)[:])
        early_gaps = keep.tile(
            [P, 4, EARLY.stop], F32, name="early_gaps", tag=f"other{POOL_TILES - 1}_0", align_bytes=64
        )
        pick_gap(POOL_TILES, EARLY, early_gaps[:, POOL_TILES - 4, :])
        for k in range(POOL_TILES + 1, ROW_TILES):
            pick_gap(k, EARLY, early_gaps[:, k - 4, :])
            clip(k - 1, EARLY)
            respond(k - 1, EARLY, bank(k - 5, [P, early_blocks, P])[:], turned_early)
        for c in range(0, N, P):
            nc.scalar.copy(
                w2_grouped[1][:, c : c + P, :].rearrange("p (c i) t -> p c t i", i=4),
                w2_raw[2 + c // (N // 2)][:, :, c % (N // 2) : c % (N // 2) + P].rearrange("p t (c i) -> p c t i", i=4),
            )
        late_owns = placed("late_owns", [P, 4, P], F32, POOLED_AT)
        pick_own(4, LATE, late_owns[:, 0, :])
        clip(7, EARLY)
        pair = psum.tile([P, 2, 4, P], F32, name="pair", offset=BANK_BYTES * 4)
        respond(7, EARLY, pair[:, 0, 0:early_blocks, :], turned_early)
        for k in range(5, ROW_TILES):
            pick_own(k, LATE, late_owns[:, k - 4, :])
        early_z = [
            turn_back(1, turned_early, EARLY, 0, 2, 6, nc.scalar.copy),
            turn_back(1, turned_early, EARLY, 2, 1, 7, nc.scalar.copy),
        ]

        pick_gap(4, LATE, piece("gap", 4, LATE)[:])
        for k in range(5, ROW_TILES):
            gap = placed("last_gap", [P, P], F32, LAST_GAP_AT) if k == ROW_TILES - 1 else piece("gap", k, LATE)
            pick_gap(k, LATE, gap[:])
            clip(k - 1, LATE)
        three = bank(5, [P, 3, P])
        for n, terms in enumerate((owns, cuts)):
            for k in range(4, 7):
                turn(three[:, k - 4, :], terms[k, LATE.start], n == 0 and k == 4, n == 1 and k == 6)
        nc.scalar.activation(
            turned_late[:, :, 0, 0 : 3 * 64].rearrange("m u (q e) -> m u q e", e=2),
            three[:].rearrange("m t (q u e) -> m u (t q) e", u=2, e=2),
            ACT.Exp,
            scale=-1.0,
        )
        clip(7, LATE)
        wide = psum.tile([P, 4, 4, P], F32, name="wide", offset=BANK_BYTES)
        respond(7, LATE, wide[:, 3, 0:1, :], turned_late)
        for made in first_z:
            quantize_z(*made)
        quantize_w2(0, placed("w2_planes", [P, N], U8, LAST_GAP_AT + 2 * P))
        quantize_z(*early_z[0])
        late_z = turn_back(1, turned_late, LATE, 0, 1, 0, nc.scalar.copy)
        quantize_z(*early_z[1])
        quantize_z(*late_z)
        warm_root = keep.tile([P, 8], F32, name="warm_root", tag=f"turned1_{LATE.start}")
        nc.scalar.activation(warm_root[:, 0:1], log_gain[:, 0:1], ACT.Abs_reciprocal_sqrt, bias=1.0)
        quantize_w2(1, keep.tile([P, N], U8, name="w2_right", tag=f"z1_{LATE.start}", align_bytes=64))

        accs = [bank(j + 1, [P, SHARES]) for j in range(N // P)]
        for j in range(N // P):
            for b in range(2):
                nc.tensor.matmul_mx(
                    out=accs[j][:],
                    lhsT=w2_w[b][:, P * j : P * (j + 1)].bitcast(FP8X4),
                    lhsT_scale=w2_planes[j // 2][:, N // 2 * b + P * (j % 2) : N // 2 * b + P * (j % 2 + 1)],
                    rhs=z_w[b][:].bitcast(FP8X4),
                    rhs_scale=z_sc[b],
                    start=(b == 0),
                    stop=(b == 1),
                )

        ys, sizes, roots, damps = {}, {}, {}, {}

        def leave(j, copy, tag):
            ys[j] = keep.tile([P, SHARES], F32, name="y", tag=tag)
            copy(ys[j][:], accs[j][:])

        def parts(j):
            return [slice(0, P), slice(P, PAIRS)] if j == N // P - 1 else [slice(0, PAIRS)]

        def size(j):
            right = keep.tile([P, PAIRS], F32, name="right", tag=f"right{j}")
            nc.vector.tensor_copy(right[:], ys[j][:].indirect(pos4_t[:]))
            sizes[j] = keep.tile([P, PAIRS], F32, name=f"size{j}")
            nc.scalar.activation(sizes[j][:], right[:], ACT.Abs)

        def root(j):
            roots[j] = keep.tile([P, PAIRS], F32, name=f"root{j}")
            for cols in parts(j):
                nc.scalar.activation(roots[j][:, cols], sizes[j][:, cols], ACT.Abs_reciprocal_sqrt, bias=1.0)

        def damp(j):
            damps[j] = keep.tile([P, PAIRS], F32, name=f"damp{j}")
            for cols in parts(j):
                nc.scalar.activation(damps[j][:, cols], roots[j][:, cols], ACT.Square)

        leave(0, nc.vector.tensor_copy, "y0")
        leave(1, nc.scalar.copy, "y1")
        leave(2, nc.scalar.copy, "y2")
        size(0)
        size(1)
        leave(3, nc.vector.tensor_copy, "right0")
        root(0)
        root(1)
        damp(0)
        size(2)
        damp(1)
        root(2)
        size(3)
        damp(2)
        root(3)
        damp(3)
        for j in range(N // P):
            res = keep.tile([P, PAIRS], F32, name=f"res{j}")
            for cols in parts(j):
                left = ys[j][:].indirect(entries(pos3_t, cols))
                nc.vector.tensor_tensor(res[:, cols], left, damps[j][:, cols], ALU.mult)
                nc.sync.dma_start(out[P * j : P * (j + 1), cols], res[:, cols])
